import numpy as np
import ml_dtypes


def mxq(x, axis, fmt="e4m3"):
    dtype, down = {"e4m3": (ml_dtypes.float8_e4m3fn, 7), "e5m2": (ml_dtypes.float8_e5m2, 14)}[fmt]
    v = np.moveaxis(np.asarray(x, np.float32).astype(ml_dtypes.bfloat16).astype(np.float64), axis, -1)
    blocks = v.reshape(v.shape[:-1] + (-1, 32))
    amax = np.abs(blocks).max(-1, keepdims=True)
    byte = np.maximum(np.where(amax > 0, np.frexp(amax)[1] - 1 + 127, 0) - down, 1)
    scale = np.exp2(byte - 127.0)
    codes = (blocks / scale).astype(np.float32).astype(dtype).astype(np.float64)
    return np.moveaxis((codes * scale).reshape(v.shape), -1, axis)


WIDE = False


def mx_kscale(k):
    if not WIDE:
        return np.ones(k)
    levels = np.array([10, -10, 5, -5, 0])
    if k % 512:
        return np.exp2(np.random.permutation(np.resize(levels, k // 32))).repeat(32)
    a = np.empty((k // 512, 16))
    for p in range(k // 512):
        a[p, :8] = np.random.permutation(np.resize(levels, 8))
        for g in range(8):
            far = levels[np.abs(levels - a[p, g]) >= 10]
            a[p, g + 8] = far[np.random.randint(len(far))]
    return np.exp2(a.ravel()).repeat(32)


def f64(x):
    return np.asarray(x).astype(np.float64)


def striped(idx):
    return np.tile(idx.reshape(-1, 16).T, (8, 1)).astype(np.uint16)


def unstriped(offs):
    return offs[:16].T.reshape(-1).astype(np.int64)


E2M1 = np.array([0.0, 0.5, 1.0, 1.5, 2.0, 3.0, 4.0, 6.0, -0.0, -0.5, -1.0, -1.5, -2.0, -3.0, -4.0, -6.0])


def pack_weight(w, fmt):
    k, n = w.shape
    w = f64(np.asarray(w, np.float32).astype(ml_dtypes.bfloat16)).reshape(k // 32, 32, n)
    amax = np.abs(w).max(1)
    if fmt == "e4m3":
        byte = np.frexp(amax)[1] - 1 + 127 - 7
    else:
        mant, ex = np.frexp(amax / 6.0)
        byte = np.where(mant > 0.5, ex, ex - 1) + 127
    byte = np.clip(np.where(amax > 0, byte, 1), 1, 254)
    scaled = (w * np.exp2(127.0 - byte)[:, None, :]).reshape(k, n).astype(np.float32)
    by_word = np.ascontiguousarray(scaled.reshape(k // 512, 128, 4, n).transpose(0, 1, 3, 2))
    if fmt == "e4m3":
        words = by_word.astype(ml_dtypes.float8_e4m3fn).view(np.uint8)
    else:
        c = by_word.astype(ml_dtypes.float4_e2m1fn).view(np.uint8) & 0xF
        words = (c[..., 0::2] | (c[..., 1::2] << 4)).reshape(k // 512, 128, 2 * n)
    return np.ascontiguousarray(words), np.ascontiguousarray(byte.astype(np.uint8).reshape(k // 512, 16, n))


def unpack_weight(words, scales, fmt):
    g, _, n = scales.shape
    words = np.ascontiguousarray(words).reshape(g, 128, n, -1)
    if fmt == "e4m3":
        vals = words.view(ml_dtypes.float8_e4m3fn).astype(np.float64)
    else:
        nib = np.empty((g, 128, n, 4), np.uint8)
        nib[..., 0::2] = words & 0xF
        nib[..., 1::2] = words >> 4
        vals = E2M1[nib]
    vals = vals * np.repeat(np.exp2(scales.astype(np.float64) - 127.0), 8, axis=1)[..., None]
    return vals.transpose(0, 1, 3, 2).reshape(g * 512, n)


def gelu(v):
    return 0.5 * v * (1.0 + np.tanh(np.sqrt(2.0 / np.pi) * (v + 0.044715 * v**3)))


K, M, H, N, T, T3, S = 1024, 512, 1024, 512, 2048, 1024, 512

def setup_inputs():
    n = np.random.standard_normal
    s = mx_kscale(K)[:, None]
    sm = mx_kscale(M)[:, None]
    u = mx_kscale(H)[:, None]
    tab_words, tab_scales = pack_weight(n((K, T)) * s, "e4m3")
    tab2_words, tab2_scales = pack_weight(n((K, T)) * s, "e4m3")
    tab3_words, tab3_scales = pack_weight(n((M, T3)) * sm, "e2m1")
    w1_words, w1_scales = pack_weight(n((K, H)) / np.sqrt(K) / s, "e2m1")
    w3_words, w3_scales = pack_weight(n((M, H)) / np.sqrt(M) / sm, "e4m3")
    return {
        "tab_words": tab_words, "tab_scales": tab_scales,
        "tab2_words": tab2_words, "tab2_scales": tab2_scales,
        "tab3_words": tab3_words, "tab3_scales": tab3_scales,
        "offs": striped(np.random.permutation(T)[:S]),
        "offs2": striped(np.random.permutation(T)[:S]),
        "offs3": striped(np.random.permutation(T3)[:S]),
        "w1_words": w1_words, "w1_scales": w1_scales,
        "w2": (n((K, H)) / np.sqrt(K) / s).astype(np.float32),
        "w3_words": w3_words, "w3_scales": w3_scales,
        "gain": (np.exp(0.3 * n(H)) * u[:, 0]).astype(np.float32),
        "w4": (n((H, N)) / np.sqrt(H) / u).astype(np.float32),
    }

def reference(tab_words, tab_scales, tab2_words, tab2_scales, tab3_words, tab3_scales, offs, offs2, offs3,
              w1_words, w1_scales, w2, w3_words, w3_scales, gain, w4):
    v = unpack_weight(tab_words, tab_scales, "e4m3")[:, unstriped(offs)]
    v2 = unpack_weight(tab2_words, tab2_scales, "e4m3")[:, unstriped(offs2)]
    v3 = unpack_weight(tab3_words, tab3_scales, "e2m1")[:, unstriped(offs3)]
    a = unpack_weight(w1_words, w1_scales, "e2m1").T @ v
    b = mxq(f64(w2), 0, "e4m3").T @ v2
    d = unpack_weight(w3_words, w3_scales, "e4m3").T @ v3
    h = f64(gain)[:, None] * (a * b + b * d + d * a)
    return mxq(f64(w4), 0, "e4m3").T @ mxq(h, 0, "e4m3")

@@ -1,0 +1,234 @@
+from contextlib import ExitStack
+
+import concourse.mybir as mybir
+from concourse.masks import make_identity
+
+K, M, H, N, T, T3, S = 1024, 512, 1024, 512, 2048, 1024, 512
+FLOPS = 2 * S * (2 * K * H + M * H + H * N)
+
+F32 = mybir.dt.float32
+BF16 = mybir.dt.bfloat16
+I32 = mybir.dt.int32
+U32 = mybir.dt.uint32
+U16 = mybir.dt.uint16
+U8 = mybir.dt.uint8
+FP8X4 = mybir.dt.float8_e4m3fn_x4
+FP4X4 = mybir.dt.float4_e2m1fn_x4
+MULT = mybir.AluOpType.mult
+ADD = mybir.AluOpType.add
+
+P = 128
+PACK = 4
+PASS = P * PACK
+QUADS = 4
+JT = S // P
+HB = H // PASS
+KA = K // PASS
+NT = N // P
+
+
+def tile_list_watch_chat_pairs_kernel(tc, tab_words, tab_scales, tab2_words, tab2_scales, tab3_words,
+                                                tab3_scales, offs, offs2, offs3, w1_words, w1_scales, w2,
+                                                w3_words, w3_scales, gain, w4, out):
+    nc = tc.nc
+    with ExitStack() as ctx:
+        keep = ctx.enter_context(tc.tile_pool(name="keep", bufs=1))
+        ring = ctx.enter_context(tc.tile_pool(name="ring", bufs=3))
+        psum = ctx.enter_context(tc.psum_pool(name="psum", bufs=2))
+
+        def held(name, width, dtype):
+            return keep.tile([P, width], dtype, name=name, align_bytes=64)
+
+        def zeroed_plane(name, width, engine):
+            plane = held(name, width, U8)
+            engine.memset(plane[:].bitcast(I32), 0)
+            return plane
+
+        def load_side_by_side(queue, plane, scales):
+            passes = scales.shape[0]
+            for quad in range(QUADS):
+                queue.dma_start(
+                    out=plane[32 * quad: 32 * quad + 4, :].bitcast(I32).rearrange("q (a t) -> q a t", a=passes),
+                    in_=scales[:, 4 * quad: 4 * quad + 4, :].bitcast(I32).rearrange("a q t -> q a t"))
+
+        def load_list(name, src):
+            tile = keep.tile([P, S // 16], U16, name=name)
+            nc.sync.dma_start(tile[:], src)
+            return tile
+
+        def load_words(name, src, dtype, width):
+            tile = held(name, width, dtype)
+            nc.sync.dma_start(out=tile[:].bitcast(I32), in_=src.bitcast(I32))
+            return tile
+
+        def gather(name, window, offsets, dtype):
+            picked = held(name, S, dtype)
+            nc.vector.tensor_copy(picked[:], window.indirect(offsets[:]))
+            return picked
+
+        v3_sc = zeroed_plane("v3_sc", T3, nc.gpsimd)
+        v_sc = zeroed_plane("v_sc", KA * T, nc.vector)
+        w3_sc = zeroed_plane("w3_sc", H, nc.gpsimd)
+        w1_sc = zeroed_plane("w1_sc", KA * H, nc.vector)
+        v2_sc = zeroed_plane("v2_sc", T, nc.vector)
+
+        idx3 = load_list("idx3", offs3)
+        idx = load_list("idx", offs)
+        v3_w = load_words("v3_w", tab3_words[0], U16, T3)
+        load_side_by_side(nc.sync, v3_sc, tab3_scales)
+        v_w = [load_words("v_w0", tab_words[0].rearrange("p t i -> p (t i)"), U32, T)]
+        load_side_by_side(nc.sync, v_sc, tab_scales)
+        w3_w = load_words("w3_w", w3_words[0].rearrange("p c i -> p (c i)"), U32, H)
+        load_side_by_side(nc.sync, w3_sc, w3_scales)
+        v_w.append(load_words("v_w1", tab_words[1].rearrange("p t i -> p (t i)"), U32, T))
+        w1_w = held("w1_w", KA * H, U16)
+        nc.sync.dma_start(out=w1_w[:].bitcast(I32).rearrange("p (a c) -> p a c", a=KA),
+                          in_=w1_words.bitcast(I32).rearrange("a p c -> p a c"))
+        load_side_by_side(nc.sync, w1_sc, w1_scales)
+        v2_w = [load_words("v2_w0", tab2_words[0].rearrange("p t i -> p (t i)"), U32, T)]
+        idx2 = load_list("idx2", offs2)
+        for quad in range(QUADS):
+            nc.sync.dma_start(out=v2_sc[32 * quad: 32 * quad + 4 * KA, :].bitcast(I32),
+                              in_=tab2_scales[:, 4 * quad: 4 * quad + 4, :].bitcast(I32))
+        v2_w.append(load_words("v2_w1", tab2_words[1].rearrange("p t i -> p (t i)"), U32, T))
+        gain_sb = keep.tile([P, HB, PACK], F32, name="gain_sb")
+        nc.sync.dma_start(out=gain_sb[:], in_=gain.rearrange("(b p t) -> p b t", b=HB, t=PACK))
+
+        def load_rows(name, rows):
+            raw = keep.tile([P, PACK, PASS], F32, name=name)
+            nc.sync.dma_start(out=raw[:], in_=rows.rearrange("(p t) c -> p t c", t=PACK))
+            return raw
+
+        w2_raw = {}
+        for b in range(HB):
+            for a in range(KA):
+                w2_raw[a, b] = load_rows(f"w2_raw{a}{b}", w2[a * PASS:(a + 1) * PASS, b * PASS:(b + 1) * PASS])
+        w4_raw = [load_rows(f"w4_raw{b}", w4[b * PASS:(b + 1) * PASS, :]) for b in range(HB)]
+
+        ident = keep.tile([P, P], F32, name="ident")
+        make_identity(nc, ident[:])
+
+        def round_rows(raw):
+            grouped = ring.tile([P, PASS * PACK], BF16, name="grouped", align_bytes=64)
+            nc.scalar.copy(out=grouped[:].rearrange("p (c i t) -> p c t i", i=4, t=PACK),
+                           in_=raw[:].rearrange("p t (c i) -> p c t i", i=4))
+            return grouped
+
+        def quantise(name, grouped, width):
+            codes = held(name + "_w", width, U32)
+            plane = held(name + "_sc", width, U8)
+            nc.vector.quantize_mx(out=codes[:].bitcast(FP8X4), scales=plane[:], in_=grouped)
+            return codes, plane
+
+        g3_w = gather("g3_w", v3_w[:], idx3, U16)
+        g3_sc = gather("g3_sc", v3_sc[:], idx3, U8)
+        g_w = [gather("g_w0", v_w[0][:], idx, U32)]
+        g_sc = [gather(f"g_sc{a}", v_sc[:, a * T:(a + 1) * T], idx, U8) for a in range(KA)]
+        g_w.append(gather("g_w1", v_w[1][:], idx, U32))
+
+        def by_slot(bank):
+            return bank[:].rearrange("p (m t) -> p t m", t=PACK)
+
+        def slots(tile):
+            return tile[:].rearrange("p (t m) -> p t m", t=PACK)
+
+        sums, prods = {}, {}
+
+        d_sbs = {}
+
+        def watch(b, jt):
+            js = slice(jt * P, (jt + 1) * P)
+            rs = slice(b * PASS, (b + 1) * PASS)
+            d_ps = psum.tile([P, PASS], F32, name="d_ps", tag="d")
+            nc.tensor.matmul_mx(out=d_ps[:], lhsT=g3_w[:, js].bitcast(FP4X4), lhsT_scale=g3_sc[:, js],
+                                rhs=w3_w[:, rs].bitcast(FP8X4), rhs_scale=w3_sc[:, rs], start=True, stop=True)
+            d_sbs[b, jt] = held(f"d_sb{b}{jt}", PASS, F32)
+            nc.scalar.copy(out=slots(d_sbs[b, jt]), in_=by_slot(d_ps))
+
+        def buyer_and_watch(b, jt):
+            js = slice(jt * P, (jt + 1) * P)
+            d_sb = d_sbs[b, jt]
+            a_ps = psum.tile([P, PASS], F32, name="a_ps", tag="a")
+            for a in range(KA):
+                nc.tensor.matmul_mx(out=a_ps[:], lhsT=g_w[a][:, js].bitcast(FP8X4), lhsT_scale=g_sc[a][:, js],
+                                    rhs=w1_w[:, a * H + b * PASS: a * H + (b + 1) * PASS].bitcast(FP4X4),
+                                    rhs_scale=w1_sc[:, a * H + b * PASS: a * H + (b + 1) * PASS],
+                                    start=(a == 0), stop=(a == KA - 1))
+            sums[b, jt] = held(f"sum{b}{jt}", PASS, F32)
+            prods[b, jt] = held(f"prod{b}{jt}", PASS, F32)
+            nc.vector.tensor_tensor(out=slots(sums[b, jt]), in0=by_slot(a_ps), in1=slots(d_sb), op=ADD)
+            nc.vector.tensor_tensor(out=slots(prods[b, jt]), in0=by_slot(a_ps), in1=slots(d_sb), op=MULT)
+
+        for b in range(HB):
+            for jt in range(JT):
+                watch(b, jt)
+        crosses = {}
+
+        def seller(b, jt, w2_q):
+            js = slice(jt * P, (jt + 1) * P)
+            b_ps = psum.tile([P, PASS], F32, name="b_ps", tag="b")
+            for a in range(KA):
+                nc.tensor.matmul_mx(out=b_ps[:], lhsT=g2_w[a][:, js].bitcast(FP8X4), lhsT_scale=g2_sc[4 * a:, js],
+                                    rhs=w2_q[a][0][:].bitcast(FP8X4), rhs_scale=w2_q[a][1][:],
+                                    start=(a == 0), stop=(a == KA - 1))
+            crosses[b, jt] = ring.tile([P, PASS], F32, name="cross")
+            nc.vector.tensor_tensor(out=slots(crosses[b, jt]), in0=by_slot(b_ps), in1=slots(sums[b, jt]), op=MULT)
+
+        def combine(b, jt, h_dst):
+            t_ps = psum.tile([P, PASS], F32, name="t_ps", tag="t")
+            for t in range(PACK):
+                ms = slice(t * P, (t + 1) * P)
+                nc.tensor.matmul(out=t_ps[:, ms], lhsT=prods[b, jt][:, ms], rhs=ident[:], is_transpose=True,
+                                 start=True, stop=False)
+                nc.tensor.matmul(out=t_ps[:, ms], lhsT=crosses[b, jt][:, ms], rhs=ident[:], is_transpose=True,
+                                 start=False, stop=True)
+            nc.vector.tensor_tensor(out=h_dst.rearrange("p (j t) -> p j t", t=PACK),
+                                    in0=t_ps[:].rearrange("p (t j) -> p j t", t=PACK),
+                                    in1=gain_sb[:, b, :].unsqueeze(1).to_broadcast([P, P, PACK]), op=MULT)
+
+        for jt in range(JT):
+            buyer_and_watch(0, jt)
+        g2_sc = gather("g2_sc", v2_sc[:], idx2, U8)
+        g2_w = [gather(f"g2_w{a}", v2_w[a][:], idx2, U32) for a in range(KA)]
+        w2_q = []
+        for a in range(KA):
+            w2_q.append(quantise(f"w2q{a}0", round_rows(w2_raw[a, 0])[:], PASS))
+            buyer_and_watch(1, a)
+        h0 = held("h0", S * PACK, BF16)
+        for jt in range(JT + 1):
+            if jt < JT:
+                seller(0, jt, w2_q)
+            if jt + KA < JT:
+                buyer_and_watch(1, jt + KA)
+            if jt > 0:
+                combine(0, jt - 1, h0[:, (jt - 1) * PASS: jt * PASS])
+        w2_q = [quantise(f"w2q{a}1", round_rows(w2_raw[a, 1])[:], PASS) for a in range(KA)]
+        h0_q = quantise("h0q", h0[:], S)
+        out_v = out.rearrange("(n p) j -> p n j", p=P)
+        h1, h1_q, w4_q = {}, {}, []
+
+        def project(jt):
+            js = slice(jt * P, (jt + 1) * P)
+            o_ps = psum.tile([P, PASS], F32, name="o_ps", tag="d")
+            for nt in range(NT):
+                ns = slice(nt * P, (nt + 1) * P)
+                nc.tensor.matmul_mx(out=o_ps[:, ns], lhsT=w4_q[0][0][:, ns].bitcast(FP8X4), lhsT_scale=w4_q[0][1][:, ns],
+                                    rhs=h0_q[0][:, js].bitcast(FP8X4), rhs_scale=h0_q[1][:, js], start=True, stop=False)
+                nc.tensor.matmul_mx(out=o_ps[:, ns], lhsT=w4_q[1][0][:, ns].bitcast(FP8X4), lhsT_scale=w4_q[1][1][:, ns],
+                                    rhs=h1_q[jt][0][:].bitcast(FP8X4), rhs_scale=h1_q[jt][1][:], start=False, stop=True)
+            o_sb = ring.tile([P, PASS], F32, name="o_sb")
+            nc.scalar.copy(out=o_sb[:], in_=o_ps[:])
+            nc.sync.dma_start(out=out_v[:, :, js], in_=o_sb[:].rearrange("p (n j) -> p n j", n=NT))
+
+        for step in range(JT + 2):
+            if step < JT:
+                seller(1, step, w2_q)
+            if 0 <= step - 1 < JT:
+                h1[step - 1] = held(f"h1{step - 1}", PASS, BF16)
+                combine(1, step - 1, h1[step - 1][:])
+            if 0 <= step - 2 < JT:
+                h1_q[step - 2] = quantise(f"h1q{step - 2}", h1[step - 2][:], P)
+            if 1 <= step <= HB:
+                w4_q.append(quantise(f"w4q{step - 1}", round_rows(w4_raw[step - 1])[:], N))
+            if 0 <= step - 2 < JT:
+                project(step - 2)

@@ -51,6 +51,11 @@ def tile_list_watch_chat_pairs_kernel(tc, tab_words, tab_scales, tab2_words, tab
                     out=plane[32 * quad: 32 * quad + 4, :].bitcast(I32).rearrange("q (a t) -> q a t", a=passes),
                     in_=scales[:, 4 * quad: 4 * quad + 4, :].bitcast(I32).rearrange("a q t -> q a t"))
 
+        def load_stacked(plane, scales):
+            for quad in range(QUADS):
+                nc.sync.dma_start(out=plane[32 * quad: 32 * quad + 4 * KA, :].bitcast(I32),
+                                  in_=scales[:, 4 * quad: 4 * quad + 4, :].bitcast(I32))
+
         def load_list(name, src):
             tile = keep.tile([P, S // 16], U16, name=name)
             nc.sync.dma_start(tile[:], src)
@@ -72,45 +77,45 @@ def tile_list_watch_chat_pairs_kernel(tc, tab_words, tab_scales, tab2_words, tab
         w1_sc = zeroed_plane("w1_sc", KA * H, nc.vector)
         v2_sc = zeroed_plane("v2_sc", T, nc.vector)
 
-        idx3 = load_list("idx3", offs3)
-        idx = load_list("idx", offs)
-        v3_w = load_words("v3_w", tab3_words[0], U16, T3)
-        load_side_by_side(nc.sync, v3_sc, tab3_scales)
-        v_w = [load_words("v_w0", tab_words[0].rearrange("p t i -> p (t i)"), U32, T)]
-        load_side_by_side(nc.sync, v_sc, tab_scales)
-        w3_w = load_words("w3_w", w3_words[0].rearrange("p c i -> p (c i)"), U32, H)
-        load_side_by_side(nc.sync, w3_sc, w3_scales)
-        v_w.append(load_words("v_w1", tab_words[1].rearrange("p t i -> p (t i)"), U32, T))
-        w1_w = held("w1_w", KA * H, U16)
-        nc.sync.dma_start(out=w1_w[:].bitcast(I32).rearrange("p (a c) -> p a c", a=KA),
-                          in_=w1_words.bitcast(I32).rearrange("a p c -> p a c"))
-        load_side_by_side(nc.sync, w1_sc, w1_scales)
-        v2_w = [load_words("v2_w0", tab2_words[0].rearrange("p t i -> p (t i)"), U32, T)]
-        idx2 = load_list("idx2", offs2)
-        for quad in range(QUADS):
-            nc.sync.dma_start(out=v2_sc[32 * quad: 32 * quad + 4 * KA, :].bitcast(I32),
-                              in_=tab2_scales[:, 4 * quad: 4 * quad + 4, :].bitcast(I32))
-        v2_w.append(load_words("v2_w1", tab2_words[1].rearrange("p t i -> p (t i)"), U32, T))
-        gain_sb = keep.tile([P, HB, PACK], F32, name="gain_sb")
-        nc.sync.dma_start(out=gain_sb[:], in_=gain.rearrange("(b p t) -> p b t", b=HB, t=PACK))
-
         def load_rows(name, rows):
             raw = keep.tile([P, PACK, PASS], F32, name=name)
             nc.sync.dma_start(out=raw[:], in_=rows.rearrange("(p t) c -> p t c", t=PACK))
             return raw
 
-        w2_raw = {}
-        for b in range(HB):
-            for a in range(KA):
-                w2_raw[a, b] = load_rows(f"w2_raw{a}{b}", w2[a * PASS:(a + 1) * PASS, b * PASS:(b + 1) * PASS])
+        def load_w2(a, b):
+            return load_rows(f"w2_raw{a}{b}", w2[a * PASS:(a + 1) * PASS, b * PASS:(b + 1) * PASS])
+
+        load_side_by_side(nc.gpsimd, w3_sc, w3_scales)
+        idx3 = load_list("idx3", offs3)
+        load_side_by_side(nc.sync, v3_sc, tab3_scales)
+        v3_w = load_words("v3_w", tab3_words[0], U16, T3)
+        w3_w = load_words("w3_w", w3_words[0].rearrange("p c i -> p (c i)"), U32, H)
+        v_w = [load_words("v_w0", tab_words[0].rearrange("p t i -> p (t i)"), U32, T)]
+        idx = load_list("idx", offs)
+        load_side_by_side(nc.sync, v_sc, tab_scales)
+        v_w.append(load_words("v_w1", tab_words[1].rearrange("p t i -> p (t i)"), U32, T))
+        w1_w = held("w1_w", KA * H, U16)
+        nc.sync.dma_start(out=w1_w[:].bitcast(I32).rearrange("p (a c) -> p a c", a=KA),
+                          in_=w1_words.bitcast(I32).rearrange("a p c -> p a c"))
+        load_side_by_side(nc.sync, w1_sc, w1_scales)
+        w2_raw = {(0, 0): load_w2(0, 0)}
+        idx2 = load_list("idx2", offs2)
+        w2_raw[1, 0] = load_w2(1, 0)
+        v2_w = [load_words("v2_w0", tab2_words[0].rearrange("p t i -> p (t i)"), U32, T)]
+        load_stacked(v2_sc, tab2_scales)
+        v2_w.append(load_words("v2_w1", tab2_words[1].rearrange("p t i -> p (t i)"), U32, T))
+        gain_sb = keep.tile([P, HB, PACK], F32, name="gain_sb")
+        nc.sync.dma_start(out=gain_sb[:], in_=gain.rearrange("(b p t) -> p b t", b=HB, t=PACK))
+        for a in range(KA):
+            w2_raw[a, 1] = load_w2(a, 1)
         w4_raw = [load_rows(f"w4_raw{b}", w4[b * PASS:(b + 1) * PASS, :]) for b in range(HB)]
 
         ident = keep.tile([P, P], F32, name="ident")
         make_identity(nc, ident[:])
 
-        def round_rows(raw):
+        def round_rows(raw, copy=nc.scalar.copy):
             grouped = ring.tile([P, PASS * PACK], BF16, name="grouped", align_bytes=64)
-            nc.scalar.copy(out=grouped[:].rearrange("p (c i t) -> p c t i", i=4, t=PACK),
+            copy(out=grouped[:].rearrange("p (c i t) -> p c t i", i=4, t=PACK),
                            in_=raw[:].rearrange("p t (c i) -> p c t i", i=4))
             return grouped
 
@@ -122,9 +127,10 @@ def tile_list_watch_chat_pairs_kernel(tc, tab_words, tab_scales, tab2_words, tab
 
         g3_w = gather("g3_w", v3_w[:], idx3, U16)
         g3_sc = gather("g3_sc", v3_sc[:], idx3, U8)
-        g_w = [gather("g_w0", v_w[0][:], idx, U32)]
-        g_sc = [gather(f"g_sc{a}", v_sc[:, a * T:(a + 1) * T], idx, U8) for a in range(KA)]
-        g_w.append(gather("g_w1", v_w[1][:], idx, U32))
+        g_sc, g_w = [], []
+        for a in range(KA):
+            g_sc.append(gather(f"g_sc{a}", v_sc[:, a * T:(a + 1) * T], idx, U8))
+            g_w.append(gather(f"g_w{a}", v_w[a][:], idx, U32))
 
         def by_slot(bank):
             return bank[:].rearrange("p (m t) -> p t m", t=PACK)
@@ -156,7 +162,8 @@ def tile_list_watch_chat_pairs_kernel(tc, tab_words, tab_scales, tab2_words, tab
                                     start=(a == 0), stop=(a == KA - 1))
             sums[b, jt] = held(f"sum{b}{jt}", PASS, F32)
             prods[b, jt] = held(f"prod{b}{jt}", PASS, F32)
-            nc.vector.tensor_tensor(out=slots(sums[b, jt]), in0=by_slot(a_ps), in1=slots(d_sb), op=ADD)
+            nc.scalar.copy(out=slots(sums[b, jt]), in_=by_slot(a_ps))
+            nc.gpsimd.tensor_tensor(out=sums[b, jt][:], in0=sums[b, jt][:], in1=d_sb[:], op=ADD)
             nc.vector.tensor_tensor(out=slots(prods[b, jt]), in0=by_slot(a_ps), in1=slots(d_sb), op=MULT)
 
         for b in range(HB):
@@ -186,20 +193,20 @@ def tile_list_watch_chat_pairs_kernel(tc, tab_words, tab_scales, tab2_words, tab
                                     in0=t_ps[:].rearrange("p (t j) -> p j t", t=PACK),
                                     in1=gain_sb[:, b, :].unsqueeze(1).to_broadcast([P, P, PACK]), op=MULT)
 
-        for jt in range(JT):
-            buyer_and_watch(0, jt)
+        for b in range(HB):
+            for jt in range(JT):
+                buyer_and_watch(b, jt)
+        w2_rounded = [round_rows(w2_raw[0, 0]), round_rows(w2_raw[1, 0], nc.vector.tensor_copy)]
         g2_sc = gather("g2_sc", v2_sc[:], idx2, U8)
-        g2_w = [gather(f"g2_w{a}", v2_w[a][:], idx2, U32) for a in range(KA)]
-        w2_q = []
+        g2_w, w2_q = [], []
         for a in range(KA):
-            w2_q.append(quantise(f"w2q{a}0", round_rows(w2_raw[a, 0])[:], PASS))
-            buyer_and_watch(1, a)
+            g2_w.append(gather(f"g2_w{a}", v2_w[a][:], idx2, U32))
+            w2_q.append(quantise(f"w2q{a}0", w2_rounded[KA - 1 - a][:], PASS))
+        w2_q = w2_q[::-1]
         h0 = held("h0", S * PACK, BF16)
         for jt in range(JT + 1):
             if jt < JT:
                 seller(0, jt, w2_q)
-            if jt + KA < JT:
-                buyer_and_watch(1, jt + KA)
             if jt > 0:
                 combine(0, jt - 1, h0[:, (jt - 1) * PASS: jt * PASS])
         w2_q = [quantise(f"w2q{a}1", round_rows(w2_raw[a, 1])[:], PASS) for a in range(KA)]

@@ -21,10 +21,14 @@ P = 128
 PACK = 4
 PASS = P * PACK
 QUADS = 4
-JT = S // P
-HB = H // PASS
-KA = K // PASS
-NT = N // P
+QUAD = P // QUADS
+ROWS = 4
+LINE = 4
+BANKS = 8
+CHAT_TILES = S // P
+R_PASSES = H // PASS
+K_PASSES = K // PASS
+N_TILES = N // P
 
 
 def tile_list_watch_chat_pairs_kernel(tc, tab_words, tab_scales, tab2_words, tab2_scales, tab3_words,
@@ -34,27 +38,33 @@ def tile_list_watch_chat_pairs_kernel(tc, tab_words, tab_scales, tab2_words, tab
     with ExitStack() as ctx:
         keep = ctx.enter_context(tc.tile_pool(name="keep", bufs=1))
         ring = ctx.enter_context(tc.tile_pool(name="ring", bufs=3))
-        psum = ctx.enter_context(tc.psum_pool(name="psum", bufs=2))
+        psum = ctx.enter_context(tc.psum_pool(name="psum", bufs=BANKS))
 
         def held(name, width, dtype):
             return keep.tile([P, width], dtype, name=name, align_bytes=64)
+
+        def bank(name):
+            return psum.tile([P, PASS], F32, name=name, tag="bank")
+
+        def span(i, width):
+            return slice(i * width, (i + 1) * width)
 
         def zeroed_plane(name, width, engine):
             plane = held(name, width, U8)
             engine.memset(plane[:].bitcast(I32), 0)
             return plane
 
-        def load_side_by_side(queue, plane, scales):
+        def load_planes_side_by_side(plane, scales):
             passes = scales.shape[0]
             for quad in range(QUADS):
-                queue.dma_start(
-                    out=plane[32 * quad: 32 * quad + 4, :].bitcast(I32).rearrange("q (a t) -> q a t", a=passes),
-                    in_=scales[:, 4 * quad: 4 * quad + 4, :].bitcast(I32).rearrange("a q t -> q a t"))
+                nc.sync.dma_start(
+                    out=plane[QUAD * quad: QUAD * quad + ROWS, :].bitcast(I32).rearrange("q (a t) -> q a t", a=passes),
+                    in_=scales[:, span(quad, ROWS), :].bitcast(I32).rearrange("a q t -> q a t"))
 
-        def load_stacked(plane, scales):
+        def load_planes_stacked(plane, scales):
             for quad in range(QUADS):
-                nc.sync.dma_start(out=plane[32 * quad: 32 * quad + 4 * KA, :].bitcast(I32),
-                                  in_=scales[:, 4 * quad: 4 * quad + 4, :].bitcast(I32))
+                nc.sync.dma_start(out=plane[QUAD * quad: QUAD * quad + ROWS * K_PASSES, :].bitcast(I32),
+                                  in_=scales[:, span(quad, ROWS), :].bitcast(I32))
 
         def load_list(name, src):
             tile = keep.tile([P, S // 16], U16, name=name)
@@ -66,57 +76,26 @@ def tile_list_watch_chat_pairs_kernel(tc, tab_words, tab_scales, tab2_words, tab
             nc.sync.dma_start(out=tile[:].bitcast(I32), in_=src.bitcast(I32))
             return tile
 
-        def gather(name, window, offsets, dtype):
-            picked = held(name, S, dtype)
-            nc.vector.tensor_copy(picked[:], window.indirect(offsets[:]))
-            return picked
-
-        v3_sc = zeroed_plane("v3_sc", T3, nc.gpsimd)
-        v_sc = zeroed_plane("v_sc", KA * T, nc.vector)
-        w3_sc = zeroed_plane("w3_sc", H, nc.gpsimd)
-        w1_sc = zeroed_plane("w1_sc", KA * H, nc.vector)
-        v2_sc = zeroed_plane("v2_sc", T, nc.vector)
+        def load_fp8_words(name, src, width):
+            return load_words(name, src.rearrange("p c i -> p (c i)"), U32, width)
 
         def load_rows(name, rows):
             raw = keep.tile([P, PACK, PASS], F32, name=name)
             nc.sync.dma_start(out=raw[:], in_=rows.rearrange("(p t) c -> p t c", t=PACK))
             return raw
 
-        def load_w2(a, b):
-            return load_rows(f"w2_raw{a}{b}", w2[a * PASS:(a + 1) * PASS, b * PASS:(b + 1) * PASS])
+        def load_w2(a, half):
+            return load_rows(f"w2_raw{a}{half}", w2[span(a, PASS), span(half, PASS)])
 
-        load_side_by_side(nc.gpsimd, w3_sc, w3_scales)
-        idx3 = load_list("idx3", offs3)
-        load_side_by_side(nc.sync, v3_sc, tab3_scales)
-        v3_w = load_words("v3_w", tab3_words[0], U16, T3)
-        w3_w = load_words("w3_w", w3_words[0].rearrange("p c i -> p (c i)"), U32, H)
-        v_w = [load_words("v_w0", tab_words[0].rearrange("p t i -> p (t i)"), U32, T)]
-        idx = load_list("idx", offs)
-        load_side_by_side(nc.sync, v_sc, tab_scales)
-        v_w.append(load_words("v_w1", tab_words[1].rearrange("p t i -> p (t i)"), U32, T))
-        w1_w = held("w1_w", KA * H, U16)
-        nc.sync.dma_start(out=w1_w[:].bitcast(I32).rearrange("p (a c) -> p a c", a=KA),
-                          in_=w1_words.bitcast(I32).rearrange("a p c -> p a c"))
-        load_side_by_side(nc.sync, w1_sc, w1_scales)
-        w2_raw = {(0, 0): load_w2(0, 0)}
-        idx2 = load_list("idx2", offs2)
-        w2_raw[1, 0] = load_w2(1, 0)
-        v2_w = [load_words("v2_w0", tab2_words[0].rearrange("p t i -> p (t i)"), U32, T)]
-        load_stacked(v2_sc, tab2_scales)
-        v2_w.append(load_words("v2_w1", tab2_words[1].rearrange("p t i -> p (t i)"), U32, T))
-        gain_sb = keep.tile([P, HB, PACK], F32, name="gain_sb")
-        nc.sync.dma_start(out=gain_sb[:], in_=gain.rearrange("(b p t) -> p b t", b=HB, t=PACK))
-        for a in range(KA):
-            w2_raw[a, 1] = load_w2(a, 1)
-        w4_raw = [load_rows(f"w4_raw{b}", w4[b * PASS:(b + 1) * PASS, :]) for b in range(HB)]
+        def gather(name, window, offsets, dtype):
+            picked = held(name, S, dtype)
+            nc.vector.tensor_copy(picked[:], window.indirect(offsets[:]))
+            return picked
 
-        ident = keep.tile([P, P], F32, name="ident")
-        make_identity(nc, ident[:])
-
-        def round_rows(raw, copy=nc.scalar.copy):
+        def round_rows(raw, copy):
             grouped = ring.tile([P, PASS * PACK], BF16, name="grouped", align_bytes=64)
-            copy(out=grouped[:].rearrange("p (c i t) -> p c t i", i=4, t=PACK),
-                           in_=raw[:].rearrange("p t (c i) -> p c t i", i=4))
+            copy(out=grouped[:].rearrange("p (c i t) -> p c t i", i=LINE, t=PACK),
+                 in_=raw[:].rearrange("p t (c i) -> p c t i", i=LINE))
             return grouped
 
         def quantise(name, grouped, width):
@@ -125,117 +104,150 @@ def tile_list_watch_chat_pairs_kernel(tc, tab_words, tab_scales, tab2_words, tab
             nc.vector.quantize_mx(out=codes[:].bitcast(FP8X4), scales=plane[:], in_=grouped)
             return codes, plane
 
+        def bank_by_slot(ps):
+            return ps[:].rearrange("p (c i t) -> p c t i", i=LINE, t=PACK)
+
+        def tile_by_slot(tile):
+            return tile[:].rearrange("p (t c i) -> p c t i", t=PACK, i=LINE)
+
+        v3_sc = zeroed_plane("v3_sc", T3, nc.gpsimd)
+        v_sc = zeroed_plane("v_sc", K_PASSES * T, nc.vector)
+        w3_sc = zeroed_plane("w3_sc", H, nc.gpsimd)
+        w1_sc = zeroed_plane("w1_sc", K_PASSES * H, nc.vector)
+        v2_sc = zeroed_plane("v2_sc", T, nc.vector)
+
+        idx3 = load_list("idx3", offs3)
+        idx = load_list("idx", offs)
+        v3_w = load_words("v3_w", tab3_words[0], U16, T3)
+        load_planes_side_by_side(v3_sc, tab3_scales)
+        v_w = [load_fp8_words("v_w0", tab_words[0], T)]
+        load_planes_side_by_side(v_sc, tab_scales)
+        w3_w = load_fp8_words("w3_w", w3_words[0], H)
+        load_planes_side_by_side(w3_sc, w3_scales)
+        v_w.append(load_fp8_words("v_w1", tab_words[1], T))
+        w1_w = held("w1_w", K_PASSES * H, U16)
+        nc.sync.dma_start(out=w1_w[:].bitcast(I32).rearrange("p (a c) -> p a c", a=K_PASSES),
+                          in_=w1_words.bitcast(I32).rearrange("a p c -> p a c"))
+        load_planes_side_by_side(w1_sc, w1_scales)
+        v2_w = [load_fp8_words("v2_w0", tab2_words[0], T)]
+        idx2 = load_list("idx2", offs2)
+        load_planes_stacked(v2_sc, tab2_scales)
+        w2_raw = {(0, 0): load_w2(0, 0)}
+        v2_w.append(load_fp8_words("v2_w1", tab2_words[1], T))
+        gain_sb = keep.tile([P, R_PASSES, PACK], F32, name="gain_sb")
+        nc.sync.dma_start(out=gain_sb[:], in_=gain.rearrange("(h p t) -> p h t", h=R_PASSES, t=PACK))
+        w2_raw[1, 0] = load_w2(1, 0)
+        for a in range(K_PASSES):
+            w2_raw[a, 1] = load_w2(a, 1)
+        w4_raw = [load_rows(f"w4_raw{half}", w4[span(half, PASS), :]) for half in range(R_PASSES)]
+
+        ident = keep.tile([P, P], F32, name="ident")
+        make_identity(nc, ident[:])
+
         g3_w = gather("g3_w", v3_w[:], idx3, U16)
         g3_sc = gather("g3_sc", v3_sc[:], idx3, U8)
         g_sc, g_w = [], []
-        for a in range(KA):
-            g_sc.append(gather(f"g_sc{a}", v_sc[:, a * T:(a + 1) * T], idx, U8))
+        for a in range(K_PASSES):
+            g_sc.append(gather(f"g_sc{a}", v_sc[:, span(a, T)], idx, U8))
             g_w.append(gather(f"g_w{a}", v_w[a][:], idx, U32))
 
-        def by_slot(bank):
-            return bank[:].rearrange("p (m t) -> p t m", t=PACK)
+        d_sb, a_plus_d, a_times_d, b_times_sum = {}, {}, {}, {}
 
-        def slots(tile):
-            return tile[:].rearrange("p (t m) -> p t m", t=PACK)
-
-        sums, prods = {}, {}
-
-        d_sbs = {}
-
-        def watch(b, jt):
-            js = slice(jt * P, (jt + 1) * P)
-            rs = slice(b * PASS, (b + 1) * PASS)
-            d_ps = psum.tile([P, PASS], F32, name="d_ps", tag="d")
+        def watch(half, jt):
+            js, rs = span(jt, P), span(half, PASS)
+            d_ps = bank("d_ps")
             nc.tensor.matmul_mx(out=d_ps[:], lhsT=g3_w[:, js].bitcast(FP4X4), lhsT_scale=g3_sc[:, js],
                                 rhs=w3_w[:, rs].bitcast(FP8X4), rhs_scale=w3_sc[:, rs], start=True, stop=True)
-            d_sbs[b, jt] = held(f"d_sb{b}{jt}", PASS, F32)
-            nc.scalar.copy(out=slots(d_sbs[b, jt]), in_=by_slot(d_ps))
+            d_sb[half, jt] = held(f"d_sb{half}{jt}", PASS, F32)
+            nc.scalar.copy(out=tile_by_slot(d_sb[half, jt]), in_=bank_by_slot(d_ps))
 
-        def buyer_and_watch(b, jt):
-            js = slice(jt * P, (jt + 1) * P)
-            d_sb = d_sbs[b, jt]
-            a_ps = psum.tile([P, PASS], F32, name="a_ps", tag="a")
-            for a in range(KA):
+        def buyer(half, jt):
+            js = span(jt, P)
+            a_ps = bank("a_ps")
+            for a in range(K_PASSES):
+                rs = span(a * R_PASSES + half, PASS)
                 nc.tensor.matmul_mx(out=a_ps[:], lhsT=g_w[a][:, js].bitcast(FP8X4), lhsT_scale=g_sc[a][:, js],
-                                    rhs=w1_w[:, a * H + b * PASS: a * H + (b + 1) * PASS].bitcast(FP4X4),
-                                    rhs_scale=w1_sc[:, a * H + b * PASS: a * H + (b + 1) * PASS],
-                                    start=(a == 0), stop=(a == KA - 1))
-            sums[b, jt] = held(f"sum{b}{jt}", PASS, F32)
-            prods[b, jt] = held(f"prod{b}{jt}", PASS, F32)
-            nc.scalar.copy(out=slots(sums[b, jt]), in_=by_slot(a_ps))
-            nc.gpsimd.tensor_tensor(out=sums[b, jt][:], in0=sums[b, jt][:], in1=d_sb[:], op=ADD)
-            nc.vector.tensor_tensor(out=slots(prods[b, jt]), in0=by_slot(a_ps), in1=slots(d_sb), op=MULT)
+                                    rhs=w1_w[:, rs].bitcast(FP4X4), rhs_scale=w1_sc[:, rs],
+                                    start=(a == 0), stop=(a == K_PASSES - 1))
+            total = held(f"a_plus_d{half}{jt}", PASS, F32)
+            product = held(f"a_times_d{half}{jt}", PASS, F32)
+            nc.vector.tensor_tensor(out=tile_by_slot(product), in0=bank_by_slot(a_ps),
+                                    in1=tile_by_slot(d_sb[half, jt]), op=MULT)
+            nc.scalar.copy(out=tile_by_slot(total), in_=bank_by_slot(a_ps))
+            nc.gpsimd.tensor_tensor(out=total[:], in0=total[:], in1=d_sb[half, jt][:], op=ADD)
+            a_plus_d[half, jt], a_times_d[half, jt] = total, product
 
-        for b in range(HB):
-            for jt in range(JT):
-                watch(b, jt)
-        crosses = {}
-
-        def seller(b, jt, w2_q):
-            js = slice(jt * P, (jt + 1) * P)
-            b_ps = psum.tile([P, PASS], F32, name="b_ps", tag="b")
-            for a in range(KA):
-                nc.tensor.matmul_mx(out=b_ps[:], lhsT=g2_w[a][:, js].bitcast(FP8X4), lhsT_scale=g2_sc[4 * a:, js],
+        def seller(half, jt, w2_q):
+            js = span(jt, P)
+            b_ps = bank("b_ps")
+            for a in range(K_PASSES):
+                nc.tensor.matmul_mx(out=b_ps[:], lhsT=g2_w[a][:, js].bitcast(FP8X4), lhsT_scale=g2_sc[ROWS * a:, js],
                                     rhs=w2_q[a][0][:].bitcast(FP8X4), rhs_scale=w2_q[a][1][:],
-                                    start=(a == 0), stop=(a == KA - 1))
-            crosses[b, jt] = ring.tile([P, PASS], F32, name="cross")
-            nc.vector.tensor_tensor(out=slots(crosses[b, jt]), in0=by_slot(b_ps), in1=slots(sums[b, jt]), op=MULT)
+                                    start=(a == 0), stop=(a == K_PASSES - 1))
+            product = ring.tile([P, PASS], F32, name="b_times_sum", bufs=CHAT_TILES)
+            nc.vector.tensor_tensor(out=tile_by_slot(product), in0=bank_by_slot(b_ps),
+                                    in1=tile_by_slot(a_plus_d[half, jt]), op=MULT)
+            b_times_sum[half, jt] = product
 
-        def combine(b, jt, h_dst):
-            t_ps = psum.tile([P, PASS], F32, name="t_ps", tag="t")
+        def combine(half, jt, h_dst):
+            h_ps = bank("h_ps")
             for t in range(PACK):
-                ms = slice(t * P, (t + 1) * P)
-                nc.tensor.matmul(out=t_ps[:, ms], lhsT=prods[b, jt][:, ms], rhs=ident[:], is_transpose=True,
+                ms = span(t, P)
+                nc.tensor.matmul(out=h_ps[:, ms], lhsT=a_times_d[half, jt][:, ms], rhs=ident[:], is_transpose=True,
                                  start=True, stop=False)
-                nc.tensor.matmul(out=t_ps[:, ms], lhsT=crosses[b, jt][:, ms], rhs=ident[:], is_transpose=True,
+                nc.tensor.matmul(out=h_ps[:, ms], lhsT=b_times_sum[half, jt][:, ms], rhs=ident[:], is_transpose=True,
                                  start=False, stop=True)
             nc.vector.tensor_tensor(out=h_dst.rearrange("p (j t) -> p j t", t=PACK),
-                                    in0=t_ps[:].rearrange("p (t j) -> p j t", t=PACK),
-                                    in1=gain_sb[:, b, :].unsqueeze(1).to_broadcast([P, P, PACK]), op=MULT)
+                                    in0=h_ps[:].rearrange("p (t j) -> p j t", t=PACK),
+                                    in1=gain_sb[:, half, :].unsqueeze(1).to_broadcast([P, P, PACK]), op=MULT)
 
-        for b in range(HB):
-            for jt in range(JT):
-                buyer_and_watch(b, jt)
-        w2_rounded = [round_rows(w2_raw[0, 0]), round_rows(w2_raw[1, 0], nc.vector.tensor_copy)]
+        for stage in (watch, buyer):
+            for half in range(R_PASSES):
+                for jt in range(CHAT_TILES):
+                    stage(half, jt)
+
+        w2_rounded = [round_rows(w2_raw[0, 0], nc.vector.tensor_copy), round_rows(w2_raw[1, 0], nc.scalar.copy)]
+        g2_w = [gather("g2_w0", v2_w[0][:], idx2, U32)]
         g2_sc = gather("g2_sc", v2_sc[:], idx2, U8)
-        g2_w, w2_q = [], []
-        for a in range(KA):
-            g2_w.append(gather(f"g2_w{a}", v2_w[a][:], idx2, U32))
-            w2_q.append(quantise(f"w2q{a}0", w2_rounded[KA - 1 - a][:], PASS))
-        w2_q = w2_q[::-1]
-        h0 = held("h0", S * PACK, BF16)
-        for jt in range(JT + 1):
-            if jt < JT:
-                seller(0, jt, w2_q)
-            if jt > 0:
-                combine(0, jt - 1, h0[:, (jt - 1) * PASS: jt * PASS])
-        w2_q = [quantise(f"w2q{a}1", round_rows(w2_raw[a, 1])[:], PASS) for a in range(KA)]
-        h0_q = quantise("h0q", h0[:], S)
+        g2_w.append(gather("g2_w1", v2_w[1][:], idx2, U32))
+
+        w2_q = [quantise(f"w2_q{a}0", w2_rounded[a][:], PASS) for a in range(K_PASSES)]
+        h_first = held("h_first", S * PACK, BF16)
+        for step in range(CHAT_TILES + 1):
+            if step < CHAT_TILES:
+                seller(0, step, w2_q)
+            if step > 0:
+                combine(0, step - 1, h_first[:, span(step - 1, PASS)])
+        w2_q = [quantise(f"w2_q{a}1", round_rows(w2_raw[a, 1], nc.scalar.copy)[:], PASS) for a in range(K_PASSES)]
+        h_first_q = quantise("h_first_q", h_first[:], S)
+
         out_v = out.rearrange("(n p) j -> p n j", p=P)
-        h1, h1_q, w4_q = {}, {}, []
+        h_second, h_second_q, w4_q = {}, {}, []
 
         def project(jt):
-            js = slice(jt * P, (jt + 1) * P)
-            o_ps = psum.tile([P, PASS], F32, name="o_ps", tag="d")
-            for nt in range(NT):
-                ns = slice(nt * P, (nt + 1) * P)
-                nc.tensor.matmul_mx(out=o_ps[:, ns], lhsT=w4_q[0][0][:, ns].bitcast(FP8X4), lhsT_scale=w4_q[0][1][:, ns],
-                                    rhs=h0_q[0][:, js].bitcast(FP8X4), rhs_scale=h0_q[1][:, js], start=True, stop=False)
-                nc.tensor.matmul_mx(out=o_ps[:, ns], lhsT=w4_q[1][0][:, ns].bitcast(FP8X4), lhsT_scale=w4_q[1][1][:, ns],
-                                    rhs=h1_q[jt][0][:].bitcast(FP8X4), rhs_scale=h1_q[jt][1][:], start=False, stop=True)
-            o_sb = ring.tile([P, PASS], F32, name="o_sb")
+            js = span(jt, P)
+            o_ps = bank("o_ps")
+            moving = ((h_first_q[0][:, js], h_first_q[1][:, js]), (h_second_q[jt][0][:], h_second_q[jt][1][:]))
+            for half in range(R_PASSES):
+                for nt in range(N_TILES):
+                    ns = span(nt, P)
+                    nc.tensor.matmul_mx(out=o_ps[:, ns], lhsT=w4_q[half][0][:, ns].bitcast(FP8X4),
+                                        lhsT_scale=w4_q[half][1][:, ns], rhs=moving[half][0].bitcast(FP8X4),
+                                        rhs_scale=moving[half][1], start=(half == 0 and nt == 0),
+                                        stop=(half == R_PASSES - 1 and nt == N_TILES - 1))
+            o_sb = ring.tile([P, PASS], F32, name="o_sb", bufs=CHAT_TILES)
             nc.scalar.copy(out=o_sb[:], in_=o_ps[:])
-            nc.sync.dma_start(out=out_v[:, :, js], in_=o_sb[:].rearrange("p (n j) -> p n j", n=NT))
+            nc.sync.dma_start(out=out_v[:, :, js], in_=o_sb[:].rearrange("p (n j) -> p n j", n=N_TILES))
 
-        for step in range(JT + 2):
-            if step < JT:
+        for step in range(CHAT_TILES + 2):
+            if step < CHAT_TILES:
                 seller(1, step, w2_q)
-            if 0 <= step - 1 < JT:
-                h1[step - 1] = held(f"h1{step - 1}", PASS, BF16)
-                combine(1, step - 1, h1[step - 1][:])
-            if 0 <= step - 2 < JT:
-                h1_q[step - 2] = quantise(f"h1q{step - 2}", h1[step - 2][:], P)
-            if 1 <= step <= HB:
-                w4_q.append(quantise(f"w4q{step - 1}", round_rows(w4_raw[step - 1])[:], N))
-            if 0 <= step - 2 < JT:
+            if 1 <= step <= CHAT_TILES:
+                h_second[step - 1] = held(f"h_second{step - 1}", PASS, BF16)
+                combine(1, step - 1, h_second[step - 1][:])
+            if step >= 2:
+                h_second_q[step - 2] = quantise(f"h_second_q{step - 2}", h_second[step - 2][:], P)
+            if 1 <= step <= R_PASSES:
+                w4_q.append(quantise(f"w4_q{step - 1}", round_rows(w4_raw[step - 1], nc.scalar.copy)[:], N))
+            if step >= 2:
                 project(step - 2)

@@ -23,25 +23,27 @@ PASS = P * PACK
 QUADS = 4
 QUAD = P // QUADS
 ROWS = 4
+RUN = 8
+GROUPS = P // RUN
 LINE = 4
 BANKS = 8
-CHAT_TILES = S // P
 R_PASSES = H // PASS
 K_PASSES = K // PASS
 N_TILES = N // P
+CHAT_PARTS = 2
+CHATS = S // CHAT_PARTS
 
 
 def tile_list_watch_chat_pairs_kernel(tc, tab_words, tab_scales, tab2_words, tab2_scales, tab3_words,
-                                                tab3_scales, offs, offs2, offs3, w1_words, w1_scales, w2,
-                                                w3_words, w3_scales, gain, w4, out):
+                                                    tab3_scales, offs, offs2, offs3, w1_words, w1_scales, w2,
+                                                    w3_words, w3_scales, gain, w4, out):
     nc = tc.nc
     with ExitStack() as ctx:
         keep = ctx.enter_context(tc.tile_pool(name="keep", bufs=1))
-        ring = ctx.enter_context(tc.tile_pool(name="ring", bufs=3))
         psum = ctx.enter_context(tc.psum_pool(name="psum", bufs=BANKS))
 
-        def held(name, width, dtype):
-            return keep.tile([P, width], dtype, name=name, align_bytes=64)
+        def held(name, width, dtype, room=None):
+            return keep.tile([P, width], dtype, name=name, tag=room or name, align_bytes=64)
 
         def bank(name):
             return psum.tile([P, PASS], F32, name=name, tag="bank")
@@ -54,10 +56,10 @@ def tile_list_watch_chat_pairs_kernel(tc, tab_words, tab_scales, tab2_words, tab
             engine.memset(plane[:].bitcast(I32), 0)
             return plane
 
-        def load_planes_side_by_side(plane, scales):
+        def load_planes_side_by_side(plane, scales, queue):
             passes = scales.shape[0]
             for quad in range(QUADS):
-                nc.sync.dma_start(
+                queue.dma_start(
                     out=plane[QUAD * quad: QUAD * quad + ROWS, :].bitcast(I32).rearrange("q (a t) -> q a t", a=passes),
                     in_=scales[:, span(quad, ROWS), :].bitcast(I32).rearrange("a q t -> q a t"))
 
@@ -79,175 +81,214 @@ def tile_list_watch_chat_pairs_kernel(tc, tab_words, tab_scales, tab2_words, tab
         def load_fp8_words(name, src, width):
             return load_words(name, src.rearrange("p c i -> p (c i)"), U32, width)
 
-        def load_rows(name, rows):
-            raw = keep.tile([P, PACK, PASS], F32, name=name)
-            nc.sync.dma_start(out=raw[:], in_=rows.rearrange("(p t) c -> p t c", t=PACK))
+        def load_w2(a, half):
+            raw = keep.tile([P, PACK, PASS], F32, name=f"w2_raw{a}{half}")
+            nc.sync.dma_start(out=raw[:], in_=w2[span(a, PASS), span(half, PASS)].rearrange("(p t) c -> p t c", t=PACK))
             return raw
 
-        def load_w2(a, half):
-            return load_rows(f"w2_raw{a}{half}", w2[span(a, PASS), span(half, PASS)])
+        def load_w4(half):
+            raw = keep.tile([P, PACK, N], F32, name=f"w4_raw{half}")
+            rows = w4[span(half, PASS), :].rearrange("(g t e) c -> t g e c", t=PACK, e=RUN)
+            for t in range(PACK):
+                nc.sync.dma_start(out=raw[:, t, :], in_=rows[t])
+            return raw
 
         def gather(name, window, offsets, dtype):
             picked = held(name, S, dtype)
             nc.vector.tensor_copy(picked[:], window.indirect(offsets[:]))
             return picked
 
-        def round_rows(raw, copy):
-            grouped = ring.tile([P, PASS * PACK], BF16, name="grouped", align_bytes=64)
-            copy(out=grouped[:].rearrange("p (c i t) -> p c t i", i=LINE, t=PACK),
-                 in_=raw[:].rearrange("p t (c i) -> p c t i", i=LINE))
+        def by_slot(name, src, dtype, width, words, engine):
+            dst = held(name, width, dtype)
+            engine.tensor_copy(
+                out=dst[:].bitcast(I32).rearrange("p (h t g w) -> p h t g w", t=PACK, g=GROUPS, w=words),
+                in_=src[:].bitcast(I32).rearrange("p (h g t w) -> p h t g w", t=PACK, g=GROUPS, w=words))
+            return dst
+
+        def round_w2(raw, name, room):
+            grouped = held(name, PASS * PACK, BF16, room)
+            nc.scalar.copy(out=grouped[:].rearrange("p (t g e i) -> p t g i e", t=PACK, g=GROUPS, e=RUN),
+                           in_=raw[:].rearrange("p i (g t e) -> p t g i e", t=PACK, e=RUN))
             return grouped
 
-        def quantise(name, grouped, width):
-            codes = held(name + "_w", width, U32)
+        def round_w4(raw, name):
+            grouped = held(name, PASS * PACK, BF16)
+            nc.scalar.copy(out=grouped[:].rearrange("p (c i t) -> p c t i", i=LINE, t=PACK),
+                           in_=raw[:].rearrange("p t (c i) -> p c t i", i=LINE))
+            return grouped
+
+        def quantise(name, grouped, width, room=None):
+            codes = held(name + "_w", width, U32, room)
             plane = held(name + "_sc", width, U8)
             nc.vector.quantize_mx(out=codes[:].bitcast(FP8X4), scales=plane[:], in_=grouped)
             return codes, plane
 
-        def bank_by_slot(ps):
-            return ps[:].rearrange("p (c i t) -> p c t i", i=LINE, t=PACK)
-
-        def tile_by_slot(tile):
-            return tile[:].rearrange("p (t c i) -> p c t i", t=PACK, i=LINE)
-
-        v3_sc = zeroed_plane("v3_sc", T3, nc.gpsimd)
-        v_sc = zeroed_plane("v_sc", K_PASSES * T, nc.vector)
+        v3_sc = zeroed_plane("v3_sc", T3, nc.vector)
         w3_sc = zeroed_plane("w3_sc", H, nc.gpsimd)
+        v_sc = zeroed_plane("v_sc", K_PASSES * T, nc.vector)
         w1_sc = zeroed_plane("w1_sc", K_PASSES * H, nc.vector)
         v2_sc = zeroed_plane("v2_sc", T, nc.vector)
+        gain_rows = held("gain_rows", P, F32)
+        nc.gpsimd.memset(gain_rows[:], 0.0)
 
         idx3 = load_list("idx3", offs3)
-        idx = load_list("idx", offs)
         v3_w = load_words("v3_w", tab3_words[0], U16, T3)
-        load_planes_side_by_side(v3_sc, tab3_scales)
-        v_w = [load_fp8_words("v_w0", tab_words[0], T)]
-        load_planes_side_by_side(v_sc, tab_scales)
+        load_planes_side_by_side(v3_sc, tab3_scales, nc.sync)
         w3_w = load_fp8_words("w3_w", w3_words[0], H)
-        load_planes_side_by_side(w3_sc, w3_scales)
-        v_w.append(load_fp8_words("v_w1", tab_words[1], T))
+        v_w = [load_fp8_words("v_w0", tab_words[0], T)]
+        idx = load_list("idx", offs)
+        load_planes_side_by_side(w3_sc, w3_scales, nc.sync)
         w1_w = held("w1_w", K_PASSES * H, U16)
         nc.sync.dma_start(out=w1_w[:].bitcast(I32).rearrange("p (a c) -> p a c", a=K_PASSES),
                           in_=w1_words.bitcast(I32).rearrange("a p c -> p a c"))
-        load_planes_side_by_side(w1_sc, w1_scales)
+        v_w.append(load_fp8_words("v_w1", tab_words[1], T))
+        load_planes_side_by_side(v_sc, tab_scales, nc.sync)
+        w2_raw = {(0, 0): load_w2(0, 0)}
+        load_planes_side_by_side(w1_sc, w1_scales, nc.sync)
+        for half in range(R_PASSES):
+            nc.sync.dma_start(
+                out=gain_rows[span(half, PACK), :].rearrange("t (g e) -> t g e", e=RUN),
+                in_=gain[span(half, PASS)].rearrange("(g t e) -> t g e", t=PACK, e=RUN))
+        w2_raw[1, 0] = load_w2(1, 0)
         v2_w = [load_fp8_words("v2_w0", tab2_words[0], T)]
         idx2 = load_list("idx2", offs2)
         load_planes_stacked(v2_sc, tab2_scales)
-        w2_raw = {(0, 0): load_w2(0, 0)}
         v2_w.append(load_fp8_words("v2_w1", tab2_words[1], T))
-        gain_sb = keep.tile([P, R_PASSES, PACK], F32, name="gain_sb")
-        nc.sync.dma_start(out=gain_sb[:], in_=gain.rearrange("(h p t) -> p h t", h=R_PASSES, t=PACK))
-        w2_raw[1, 0] = load_w2(1, 0)
         for a in range(K_PASSES):
             w2_raw[a, 1] = load_w2(a, 1)
-        w4_raw = [load_rows(f"w4_raw{half}", w4[span(half, PASS), :]) for half in range(R_PASSES)]
+        w4_raw = [load_w4(half) for half in range(R_PASSES)]
 
         ident = keep.tile([P, P], F32, name="ident")
         make_identity(nc, ident[:])
 
         g3_w = gather("g3_w", v3_w[:], idx3, U16)
         g3_sc = gather("g3_sc", v3_sc[:], idx3, U8)
-        g_sc, g_w = [], []
-        for a in range(K_PASSES):
-            g_sc.append(gather(f"g_sc{a}", v_sc[:, span(a, T)], idx, U8))
-            g_w.append(gather(f"g_w{a}", v_w[a][:], idx, U32))
+        w3_wo = by_slot("w3_wo", w3_w, U32, H, RUN, nc.gpsimd)
+        w3_so = by_slot("w3_so", w3_sc, U8, H, RUN // 4, nc.gpsimd)
+        g_w = [gather("g_w0", v_w[0][:], idx, U32)]
+        w1_wo = by_slot("w1_wo", w1_w, U16, K_PASSES * H, RUN // 2, nc.gpsimd)
+        g_w.append(gather("g_w1", v_w[1][:], idx, U32))
+        g_sc = [gather(f"g_sc{a}", v_sc[:, span(a, T)], idx, U8) for a in range(K_PASSES)]
+        w1_so = by_slot("w1_so", w1_sc, U8, K_PASSES * H, RUN // 4, nc.vector)
 
-        d_sb, a_plus_d, a_times_d, b_times_sum = {}, {}, {}, {}
+        d_sb = [keep.tile([P, PACK, S], F32, name=f"d_sb{half}") for half in range(R_PASSES)]
+        a_plus_d = [keep.tile([P, PACK, S], F32, name="a_plus_d0", tag="w2_raw10"),
+                    keep.tile([P, PACK, S], F32, name="a_plus_d1")]
+        a_times_d = {}
 
-        def watch(half, jt):
-            js, rs = span(jt, P), span(half, PASS)
-            d_ps = bank("d_ps")
-            nc.tensor.matmul_mx(out=d_ps[:], lhsT=g3_w[:, js].bitcast(FP4X4), lhsT_scale=g3_sc[:, js],
-                                rhs=w3_w[:, rs].bitcast(FP8X4), rhs_scale=w3_sc[:, rs], start=True, stop=True)
-            d_sb[half, jt] = held(f"d_sb{half}{jt}", PASS, F32)
-            nc.scalar.copy(out=tile_by_slot(d_sb[half, jt]), in_=bank_by_slot(d_ps))
+        for half in range(R_PASSES):
+            for t in range(PACK):
+                cs = span(half * PACK + t, P)
+                d_ps = bank("d_ps")
+                nc.tensor.matmul_mx(out=d_ps[:], lhsT=w3_wo[:, cs].bitcast(FP8X4), lhsT_scale=w3_so[:, cs],
+                                    rhs=g3_w[:].bitcast(FP4X4), rhs_scale=g3_sc[:], start=True, stop=True)
+                nc.scalar.copy(out=d_sb[half][:, t, :], in_=d_ps[:])
 
-        def buyer(half, jt):
-            js = span(jt, P)
+        gain_ps = bank("gain_ps")
+        nc.tensor.transpose(gain_ps[:, 0:P], gain_rows[:], ident[:])
+        gain_sb = held("gain_sb", R_PASSES * PACK, F32)
+        nc.vector.tensor_copy(out=gain_sb[:], in_=gain_ps[:, 0:R_PASSES * PACK])
+
+        def gain_of(half, t):
+            return gain_sb[:, span(half * PACK + t, 1)]
+
+        def buyer(half, t):
             a_ps = bank("a_ps")
             for a in range(K_PASSES):
-                rs = span(a * R_PASSES + half, PASS)
-                nc.tensor.matmul_mx(out=a_ps[:], lhsT=g_w[a][:, js].bitcast(FP8X4), lhsT_scale=g_sc[a][:, js],
-                                    rhs=w1_w[:, rs].bitcast(FP4X4), rhs_scale=w1_sc[:, rs],
+                nc.tensor.matmul_mx(out=a_ps[:], lhsT=w1_wo[:, span((a * R_PASSES + half) * PACK + t, P)].bitcast(FP4X4),
+                                    lhsT_scale=w1_so[:, span((a * R_PASSES + half) * PACK + t, P)],
+                                    rhs=g_w[a][:].bitcast(FP8X4), rhs_scale=g_sc[a][:],
                                     start=(a == 0), stop=(a == K_PASSES - 1))
-            total = held(f"a_plus_d{half}{jt}", PASS, F32)
-            product = held(f"a_times_d{half}{jt}", PASS, F32)
-            nc.vector.tensor_tensor(out=tile_by_slot(product), in0=bank_by_slot(a_ps),
-                                    in1=tile_by_slot(d_sb[half, jt]), op=MULT)
-            nc.scalar.copy(out=tile_by_slot(total), in_=bank_by_slot(a_ps))
-            nc.gpsimd.tensor_tensor(out=total[:], in0=total[:], in1=d_sb[half, jt][:], op=ADD)
-            a_plus_d[half, jt], a_times_d[half, jt] = total, product
+            return a_ps
 
-        def seller(half, jt, w2_q):
-            js = span(jt, P)
-            b_ps = bank("b_ps")
+        def times_d(half, t, a_ps):
+            nc.vector.scalar_tensor_tensor(out=a_times_d[half][:, t, :], in0=a_ps[:], scalar=gain_of(half, t),
+                                           in1=d_sb[half][:, t, :], op0=MULT, op1=MULT)
+
+        def plus_d(half, t, a_ps):
+            nc.scalar.copy(out=a_plus_d[half][:, t, :], in_=a_ps[:])
+            nc.gpsimd.tensor_tensor(out=a_plus_d[half][:, t, :], in0=a_plus_d[half][:, t, :],
+                                    in1=d_sb[half][:, t, :], op=ADD)
+
+        def seller(half, w2_q):
+            banks = [bank("b_ps") for t in range(PACK)]
             for a in range(K_PASSES):
-                nc.tensor.matmul_mx(out=b_ps[:], lhsT=g2_w[a][:, js].bitcast(FP8X4), lhsT_scale=g2_sc[ROWS * a:, js],
-                                    rhs=w2_q[a][0][:].bitcast(FP8X4), rhs_scale=w2_q[a][1][:],
-                                    start=(a == 0), stop=(a == K_PASSES - 1))
-            product = ring.tile([P, PASS], F32, name="b_times_sum", bufs=CHAT_TILES)
-            nc.vector.tensor_tensor(out=tile_by_slot(product), in0=bank_by_slot(b_ps),
-                                    in1=tile_by_slot(a_plus_d[half, jt]), op=MULT)
-            b_times_sum[half, jt] = product
+                for t in range(PACK):
+                    nc.tensor.matmul_mx(out=banks[t][:], lhsT=w2_q[a][0][:, span(t, P)].bitcast(FP8X4),
+                                        lhsT_scale=w2_q[a][1][:, span(t, P)], rhs=g2_w[a][:].bitcast(FP8X4),
+                                        rhs_scale=g2_sc[ROWS * a:, :], start=(a == 0), stop=(a == K_PASSES - 1))
+            return banks
 
-        def combine(half, jt, h_dst):
-            h_ps = bank("h_ps")
-            for t in range(PACK):
-                ms = span(t, P)
-                nc.tensor.matmul(out=h_ps[:, ms], lhsT=a_times_d[half, jt][:, ms], rhs=ident[:], is_transpose=True,
-                                 start=True, stop=False)
-                nc.tensor.matmul(out=h_ps[:, ms], lhsT=b_times_sum[half, jt][:, ms], rhs=ident[:], is_transpose=True,
-                                 start=False, stop=True)
-            nc.vector.tensor_tensor(out=h_dst.rearrange("p (j t) -> p j t", t=PACK),
-                                    in0=h_ps[:].rearrange("p (t j) -> p j t", t=PACK),
-                                    in1=gain_sb[:, half, :].unsqueeze(1).to_broadcast([P, P, PACK]), op=MULT)
+        w2_bf = {(a, 0): round_w2(w2_raw[a, 0], f"w2_bf{a}0", None) for a in range(K_PASSES)}
+        a_times_d[0] = keep.tile([P, PACK, S], F32, name="a_times_d0")
+        for t in range(PACK):
+            a_ps = buyer(0, t)
+            times_d(0, t, a_ps)
+            plus_d(0, t, a_ps)
+        a_second = [buyer(1, t) for t in range(PACK)]
+        for t in range(PACK):
+            plus_d(1, t, a_second[t])
 
-        for stage in (watch, buyer):
-            for half in range(R_PASSES):
-                for jt in range(CHAT_TILES):
-                    stage(half, jt)
-
-        w2_rounded = [round_rows(w2_raw[0, 0], nc.vector.tensor_copy), round_rows(w2_raw[1, 0], nc.scalar.copy)]
+        w2_q = [quantise("w2_q00", w2_bf[0, 0][:], PASS, "w1_sc"), quantise("w2_q10", w2_bf[1, 0][:], PASS)]
         g2_w = [gather("g2_w0", v2_w[0][:], idx2, U32)]
         g2_sc = gather("g2_sc", v2_sc[:], idx2, U8)
         g2_w.append(gather("g2_w1", v2_w[1][:], idx2, U32))
+        first_banks = seller(0, w2_q)
+        a_times_d[1] = keep.tile([P, PACK, S], F32, name="a_times_d1", tag="v2_w1", align_bytes=64)
+        for t in range(PACK):
+            times_d(1, t, a_second[t])
 
-        w2_q = [quantise(f"w2_q{a}0", w2_rounded[a][:], PASS) for a in range(K_PASSES)]
-        h_first = held("h_first", S * PACK, BF16)
-        for step in range(CHAT_TILES + 1):
-            if step < CHAT_TILES:
-                seller(0, step, w2_q)
-            if step > 0:
-                combine(0, step - 1, h_first[:, span(step - 1, PASS)])
-        w2_q = [quantise(f"w2_q{a}1", round_rows(w2_raw[a, 1], nc.scalar.copy)[:], PASS) for a in range(K_PASSES)]
-        h_first_q = quantise("h_first_q", h_first[:], S)
+        def times_sum(half, banks, js, name, room=None):
+            width = js.stop - js.start
+            product = held(name, PACK * width, F32, room)
+            for t in range(PACK):
+                nc.vector.scalar_tensor_tensor(out=product[:, span(t, width)], in0=banks[t][:, js],
+                                               scalar=gain_of(half, t), in1=a_plus_d[half][:, t, js],
+                                               op0=MULT, op1=MULT)
+            return product[:].rearrange("p (t j) -> p t j", t=PACK)
+
+        def add_up(half, product, part, engine, room=None):
+            h_bf = held(f"h_bf{half}{part}", CHATS * PACK, BF16, room)
+            engine.tensor_tensor(out=h_bf[:].rearrange("p (c i t) -> p c t i", i=LINE, t=PACK),
+                                 in0=product.rearrange("p t (c i) -> p c t i", i=LINE),
+                                 in1=a_times_d[half][:, :, span(part, CHATS)].rearrange("p t (c i) -> p c t i", i=LINE),
+                                 op=ADD)
+            return h_bf
 
         out_v = out.rearrange("(n p) j -> p n j", p=P)
-        h_second, h_second_q, w4_q = {}, {}, []
+        per_bank = PASS // CHATS
 
-        def project(jt):
-            js = span(jt, P)
-            o_ps = bank("o_ps")
-            moving = ((h_first_q[0][:, js], h_first_q[1][:, js]), (h_second_q[jt][0][:], h_second_q[jt][1][:]))
-            for half in range(R_PASSES):
-                for nt in range(N_TILES):
-                    ns = span(nt, P)
-                    nc.tensor.matmul_mx(out=o_ps[:, ns], lhsT=w4_q[half][0][:, ns].bitcast(FP8X4),
-                                        lhsT_scale=w4_q[half][1][:, ns], rhs=moving[half][0].bitcast(FP8X4),
-                                        rhs_scale=moving[half][1], start=(half == 0 and nt == 0),
-                                        stop=(half == R_PASSES - 1 and nt == N_TILES - 1))
-            o_sb = ring.tile([P, PASS], F32, name="o_sb", bufs=CHAT_TILES)
-            nc.scalar.copy(out=o_sb[:], in_=o_ps[:])
-            nc.sync.dma_start(out=out_v[:, :, js], in_=o_sb[:].rearrange("p (n j) -> p n j", n=N_TILES))
+        def project(part, moving):
+            js = span(part, CHATS)
+            for pair in range(N_TILES // per_bank):
+                o_ps = bank("o_ps")
+                for half in range(R_PASSES):
+                    for i in range(per_bank):
+                        ns = span(pair * per_bank + i, P)
+                        nc.tensor.matmul_mx(out=o_ps[:, span(i, CHATS)], lhsT=w4_q[half][0][:, ns].bitcast(FP8X4),
+                                            lhsT_scale=w4_q[half][1][:, ns], rhs=moving[half][0][:].bitcast(FP8X4),
+                                            rhs_scale=moving[half][1][:], start=(half == 0 and i == 0),
+                                            stop=(half == R_PASSES - 1 and i == per_bank - 1))
+                o_sb = held(f"o_sb{part}{pair}", PASS, F32)
+                nc.scalar.copy(out=o_sb[:], in_=o_ps[:])
+                nc.sync.dma_start(out=out_v[:, span(pair, per_bank), js],
+                                  in_=o_sb[:].rearrange("p (n j) -> p n j", n=per_bank))
 
-        for step in range(CHAT_TILES + 2):
-            if step < CHAT_TILES:
-                seller(1, step, w2_q)
-            if 1 <= step <= CHAT_TILES:
-                h_second[step - 1] = held(f"h_second{step - 1}", PASS, BF16)
-                combine(1, step - 1, h_second[step - 1][:])
-            if step >= 2:
-                h_second_q[step - 2] = quantise(f"h_second_q{step - 2}", h_second[step - 2][:], P)
-            if 1 <= step <= R_PASSES:
-                w4_q.append(quantise(f"w4_q{step - 1}", round_rows(w4_raw[step - 1], nc.scalar.copy)[:], N))
-            if step >= 2:
-                project(step - 2)
+        first_product = times_sum(0, first_banks, slice(0, S), "b_times_sum0")
+        h_bf = {(0, 0): add_up(0, first_product[:, :, span(0, CHATS)], 0, nc.gpsimd)}
+        w2_q = [quantise(f"w2_q{a}1", round_w2(w2_raw[a, 1], f"w2_bf{a}1", ("w1_w", "w3_w")[a])[:], PASS)
+                for a in range(K_PASSES)]
+        second_banks = seller(1, w2_q)
+        h_bf[0, 1] = add_up(0, first_product[:, :, span(1, CHATS)], 1, nc.vector, "w3_w")
+        w4_bf = [round_w4(w4_raw[half], f"w4_bf{half}") for half in range(R_PASSES)]
+
+        h_bf[1, 0] = add_up(1, times_sum(1, second_banks, span(0, CHATS), "b_times_sum10"), 0, nc.vector)
+        h_q = {(0, 1): quantise("h_q01", h_bf[0, 1][:], CHATS),
+               (0, 0): quantise("h_q00", h_bf[0, 0][:], CHATS, "b_times_sum10")}
+        w4_q = [quantise("w4_q0", w4_bf[0][:], N)]
+        h_q[1, 0] = quantise("h_q10", h_bf[1, 0][:], CHATS)
+        w4_q.append(quantise("w4_q1", w4_bf[1][:], N))
+        project(0, (h_q[0, 0], h_q[1, 0]))
+        h_bf[1, 1] = add_up(1, times_sum(1, second_banks, span(1, CHATS), "b_times_sum11", "w4_bf1"), 1, nc.vector)
+        h_q[1, 1] = quantise("h_q11", h_bf[1, 1][:], CHATS)
+        project(1, (h_q[0, 1], h_q[1, 1]))

@@ -163,10 +163,10 @@ def tile_list_watch_chat_pairs_kernel(tc, tab_words, tab_scales, tab2_words, tab
 
         g3_w = gather("g3_w", v3_w[:], idx3, U16)
         g3_sc = gather("g3_sc", v3_sc[:], idx3, U8)
-        w3_wo = by_slot("w3_wo", w3_w, U32, H, RUN, nc.gpsimd)
-        w3_so = by_slot("w3_so", w3_sc, U8, H, RUN // 4, nc.gpsimd)
+        w3_wo = by_slot("w3_wo", w3_w, U32, H, RUN, nc.vector)
+        w3_so = by_slot("w3_so", w3_sc, U8, H, RUN // 4, nc.vector)
         g_w = [gather("g_w0", v_w[0][:], idx, U32)]
-        w1_wo = by_slot("w1_wo", w1_w, U16, K_PASSES * H, RUN // 2, nc.gpsimd)
+        w1_wo = by_slot("w1_wo", w1_w, U16, K_PASSES * H, RUN // 2, nc.vector)
         g_w.append(gather("g_w1", v_w[1][:], idx, U32))
         g_sc = [gather(f"g_sc{a}", v_sc[:, span(a, T)], idx, U8) for a in range(K_PASSES)]
         w1_so = by_slot("w1_so", w1_sc, U8, K_PASSES * H, RUN // 4, nc.vector)
@@ -270,12 +270,15 @@ def tile_list_watch_chat_pairs_kernel(tc, tab_words, tab_scales, tab2_words, tab
                                             rhs_scale=moving[half][1][:], start=(half == 0 and i == 0),
                                             stop=(half == R_PASSES - 1 and i == per_bank - 1))
                 o_sb = held(f"o_sb{part}{pair}", PASS, F32)
-                nc.scalar.copy(out=o_sb[:], in_=o_ps[:])
+                if part == CHAT_PARTS - 1 and pair == 1:
+                    nc.vector.tensor_copy(out=o_sb[:], in_=o_ps[:])
+                else:
+                    nc.scalar.copy(out=o_sb[:], in_=o_ps[:])
                 nc.sync.dma_start(out=out_v[:, span(pair, per_bank), js],
                                   in_=o_sb[:].rearrange("p (n j) -> p n j", n=per_bank))
 
         first_product = times_sum(0, first_banks, slice(0, S), "b_times_sum0")
-        h_bf = {(0, 0): add_up(0, first_product[:, :, span(0, CHATS)], 0, nc.gpsimd)}
+        h_bf = {(0, 0): add_up(0, first_product[:, :, span(0, CHATS)], 0, nc.vector)}
         w2_q = [quantise(f"w2_q{a}1", round_w2(w2_raw[a, 1], f"w2_bf{a}1", ("w1_w", "w3_w")[a])[:], PASS)
                 for a in range(K_PASSES)]
         second_banks = seller(1, w2_q)
@@ -284,7 +287,7 @@ def tile_list_watch_chat_pairs_kernel(tc, tab_words, tab_scales, tab2_words, tab
 
         h_bf[1, 0] = add_up(1, times_sum(1, second_banks, span(0, CHATS), "b_times_sum10"), 0, nc.vector)
         h_q = {(0, 1): quantise("h_q01", h_bf[0, 1][:], CHATS),
-               (0, 0): quantise("h_q00", h_bf[0, 0][:], CHATS, "b_times_sum10")}
+               (0, 0): quantise("h_q00", h_bf[0, 0][:], CHATS)}
         w4_q = [quantise("w4_q0", w4_bf[0][:], N)]
         h_q[1, 0] = quantise("h_q10", h_bf[1, 0][:], CHATS)
         w4_q.append(quantise("w4_q1", w4_bf[1][:], N))

@@ -56,16 +56,16 @@ def tile_list_watch_chat_pairs_kernel(tc, tab_words, tab_scales, tab2_words, tab
             engine.memset(plane[:].bitcast(I32), 0)
             return plane
 
-        def load_planes_side_by_side(plane, scales, queue):
+        def load_planes_side_by_side(plane, scales):
             passes = scales.shape[0]
-            for quad in range(QUADS):
-                queue.dma_start(
-                    out=plane[QUAD * quad: QUAD * quad + ROWS, :].bitcast(I32).rearrange("q (a t) -> q a t", a=passes),
-                    in_=scales[:, span(quad, ROWS), :].bitcast(I32).rearrange("a q t -> q a t"))
+            for row in range(ROWS):
+                nc.sync.dma_start(
+                    out=plane[row:P:QUAD, :].bitcast(I32).rearrange("q (a t) -> q a t", a=passes),
+                    in_=scales[:, row:QUADS * ROWS:ROWS, :].bitcast(I32).rearrange("a q t -> q a t"))
 
         def load_planes_stacked(plane, scales):
             for quad in range(QUADS):
-                nc.sync.dma_start(out=plane[QUAD * quad: QUAD * quad + ROWS * K_PASSES, :].bitcast(I32),
+                nc.sync.dma_start(out=plane[QUAD * quad + ROWS: QUAD * quad + ROWS * (K_PASSES + 1), :].bitcast(I32),
                                   in_=scales[:, span(quad, ROWS), :].bitcast(I32))
 
         def load_list(name, src):
@@ -82,12 +82,12 @@ def tile_list_watch_chat_pairs_kernel(tc, tab_words, tab_scales, tab2_words, tab
             return load_words(name, src.rearrange("p c i -> p (c i)"), U32, width)
 
         def load_w2(a, half):
-            raw = keep.tile([P, PACK, PASS], F32, name=f"w2_raw{a}{half}")
+            raw = keep.tile([P, PACK, PASS], F32, name=f"w2_raw{a}{half}", align_bytes=64)
             nc.sync.dma_start(out=raw[:], in_=w2[span(a, PASS), span(half, PASS)].rearrange("(p t) c -> p t c", t=PACK))
             return raw
 
         def load_w4(half):
-            raw = keep.tile([P, PACK, N], F32, name=f"w4_raw{half}")
+            raw = keep.tile([P, PACK, N], F32, name=f"w4_raw{half}", align_bytes=64)
             rows = w4[span(half, PASS), :].rearrange("(g t e) c -> t g e c", t=PACK, e=RUN)
             for t in range(PACK):
                 nc.sync.dma_start(out=raw[:, t, :], in_=rows[t])
@@ -133,30 +133,31 @@ def tile_list_watch_chat_pairs_kernel(tc, tab_words, tab_scales, tab2_words, tab
 
         idx3 = load_list("idx3", offs3)
         v3_w = load_words("v3_w", tab3_words[0], U16, T3)
-        load_planes_side_by_side(v3_sc, tab3_scales, nc.sync)
+        load_planes_side_by_side(v3_sc, tab3_scales)
         w3_w = load_fp8_words("w3_w", w3_words[0], H)
-        v_w = [load_fp8_words("v_w0", tab_words[0], T)]
         idx = load_list("idx", offs)
-        load_planes_side_by_side(w3_sc, w3_scales, nc.sync)
-        w1_w = held("w1_w", K_PASSES * H, U16)
-        nc.sync.dma_start(out=w1_w[:].bitcast(I32).rearrange("p (a c) -> p a c", a=K_PASSES),
-                          in_=w1_words.bitcast(I32).rearrange("a p c -> p a c"))
+        load_planes_side_by_side(w3_sc, w3_scales)
+        v_w = [load_fp8_words("v_w0", tab_words[0], T)]
+        load_planes_side_by_side(v_sc, tab_scales)
         v_w.append(load_fp8_words("v_w1", tab_words[1], T))
-        load_planes_side_by_side(v_sc, tab_scales, nc.sync)
-        w2_raw = {(0, 0): load_w2(0, 0)}
-        load_planes_side_by_side(w1_sc, w1_scales, nc.sync)
         for half in range(R_PASSES):
             nc.sync.dma_start(
                 out=gain_rows[span(half, PACK), :].rearrange("t (g e) -> t g e", e=RUN),
                 in_=gain[span(half, PASS)].rearrange("(g t e) -> t g e", t=PACK, e=RUN))
-        w2_raw[1, 0] = load_w2(1, 0)
+        w1_w = held("w1_w", K_PASSES * H, U16)
+        nc.sync.dma_start(out=w1_w[:].bitcast(I32).rearrange("p (a c) -> p a c", a=K_PASSES),
+                          in_=w1_words.bitcast(I32).rearrange("a p c -> p a c"))
+        load_planes_side_by_side(w1_sc, w1_scales)
+        w2_raw = {(0, 0): load_w2(0, 0)}
         v2_w = [load_fp8_words("v2_w0", tab2_words[0], T)]
         idx2 = load_list("idx2", offs2)
         load_planes_stacked(v2_sc, tab2_scales)
+        w2_raw[1, 0] = load_w2(1, 0)
         v2_w.append(load_fp8_words("v2_w1", tab2_words[1], T))
-        for a in range(K_PASSES):
-            w2_raw[a, 1] = load_w2(a, 1)
-        w4_raw = [load_w4(half) for half in range(R_PASSES)]
+        w2_raw[0, 1] = load_w2(0, 1)
+        w2_raw[1, 1] = load_w2(1, 1)
+        w4_raw = [load_w4(0)]
+        w4_raw.append(load_w4(1))
 
         ident = keep.tile([P, P], F32, name="ident")
         make_identity(nc, ident[:])
@@ -166,15 +167,15 @@ def tile_list_watch_chat_pairs_kernel(tc, tab_words, tab_scales, tab2_words, tab
         w3_wo = by_slot("w3_wo", w3_w, U32, H, RUN, nc.vector)
         w3_so = by_slot("w3_so", w3_sc, U8, H, RUN // 4, nc.vector)
         g_w = [gather("g_w0", v_w[0][:], idx, U32)]
-        w1_wo = by_slot("w1_wo", w1_w, U16, K_PASSES * H, RUN // 2, nc.vector)
-        g_w.append(gather("g_w1", v_w[1][:], idx, U32))
         g_sc = [gather(f"g_sc{a}", v_sc[:, span(a, T)], idx, U8) for a in range(K_PASSES)]
+        g_w.append(gather("g_w1", v_w[1][:], idx, U32))
+        w1_wo = by_slot("w1_wo", w1_w, U16, K_PASSES * H, RUN // 2, nc.vector)
         w1_so = by_slot("w1_so", w1_sc, U8, K_PASSES * H, RUN // 4, nc.vector)
 
         d_sb = [keep.tile([P, PACK, S], F32, name=f"d_sb{half}") for half in range(R_PASSES)]
-        a_plus_d = [keep.tile([P, PACK, S], F32, name="a_plus_d0", tag="w2_raw10"),
-                    keep.tile([P, PACK, S], F32, name="a_plus_d1")]
-        a_times_d = {}
+        a_plus_d = [keep.tile([P, PACK, S], F32, name="a_plus_d0"),
+                    keep.tile([P, PACK, S], F32, name="a_plus_d1", tag="w2_raw10", align_bytes=64)]
+        a_times_d = [keep.tile([P, PACK, S], F32, name=f"a_times_d{half}") for half in range(R_PASSES)]
 
         for half in range(R_PASSES):
             for t in range(PACK):
@@ -216,43 +217,39 @@ def tile_list_watch_chat_pairs_kernel(tc, tab_words, tab_scales, tab2_words, tab
                 for t in range(PACK):
                     nc.tensor.matmul_mx(out=banks[t][:], lhsT=w2_q[a][0][:, span(t, P)].bitcast(FP8X4),
                                         lhsT_scale=w2_q[a][1][:, span(t, P)], rhs=g2_w[a][:].bitcast(FP8X4),
-                                        rhs_scale=g2_sc[ROWS * a:, :], start=(a == 0), stop=(a == K_PASSES - 1))
+                                        rhs_scale=g2_sc[ROWS * (a + 1):, :], start=(a == 0), stop=(a == K_PASSES - 1))
             return banks
 
-        w2_bf = {(a, 0): round_w2(w2_raw[a, 0], f"w2_bf{a}0", None) for a in range(K_PASSES)}
-        a_times_d[0] = keep.tile([P, PACK, S], F32, name="a_times_d0")
+        a_banks = {}
+        for half in range(R_PASSES):
+            for t in range(PACK):
+                a_banks[half, t] = buyer(half, t)
+                times_d(half, t, a_banks[half, t])
+                if half == 0:
+                    plus_d(half, t, a_banks[half, t])
+        w2_bf = [round_w2(w2_raw[0, 0], "w2_bf00", "w1_wo"), round_w2(w2_raw[1, 0], "w2_bf10", None)]
         for t in range(PACK):
-            a_ps = buyer(0, t)
-            times_d(0, t, a_ps)
-            plus_d(0, t, a_ps)
-        a_second = [buyer(1, t) for t in range(PACK)]
-        for t in range(PACK):
-            plus_d(1, t, a_second[t])
+            plus_d(1, t, a_banks[1, t])
 
-        w2_q = [quantise("w2_q00", w2_bf[0, 0][:], PASS, "w1_sc"), quantise("w2_q10", w2_bf[1, 0][:], PASS)]
         g2_w = [gather("g2_w0", v2_w[0][:], idx2, U32)]
+        w2_q = [quantise("w2_q00", w2_bf[0][:], PASS)]
         g2_sc = gather("g2_sc", v2_sc[:], idx2, U8)
+        w2_q.append(quantise("w2_q10", w2_bf[1][:], PASS))
         g2_w.append(gather("g2_w1", v2_w[1][:], idx2, U32))
         first_banks = seller(0, w2_q)
-        a_times_d[1] = keep.tile([P, PACK, S], F32, name="a_times_d1", tag="v2_w1", align_bytes=64)
-        for t in range(PACK):
-            times_d(1, t, a_second[t])
 
-        def times_sum(half, banks, js, name, room=None):
-            width = js.stop - js.start
-            product = held(name, PACK * width, F32, room)
+        def times_sum(half, banks):
+            product = keep.tile([P, PACK, S], F32, name=f"b_times_sum{half}")
             for t in range(PACK):
-                nc.vector.scalar_tensor_tensor(out=product[:, span(t, width)], in0=banks[t][:, js],
-                                               scalar=gain_of(half, t), in1=a_plus_d[half][:, t, js],
-                                               op0=MULT, op1=MULT)
-            return product[:].rearrange("p (t j) -> p t j", t=PACK)
+                nc.vector.scalar_tensor_tensor(out=product[:, t, :], in0=banks[t][:], scalar=gain_of(half, t),
+                                               in1=a_plus_d[half][:, t, :], op0=MULT, op1=MULT)
+            return product
 
-        def add_up(half, product, part, engine, room=None):
-            h_bf = held(f"h_bf{half}{part}", CHATS * PACK, BF16, room)
-            engine.tensor_tensor(out=h_bf[:].rearrange("p (c i t) -> p c t i", i=LINE, t=PACK),
-                                 in0=product.rearrange("p t (c i) -> p c t i", i=LINE),
-                                 in1=a_times_d[half][:, :, span(part, CHATS)].rearrange("p t (c i) -> p c t i", i=LINE),
-                                 op=ADD)
+        def add_up(half, product, js, room=None):
+            h_bf = held(f"h_bf{half}_{js.start}", (js.stop - js.start) * PACK, BF16, room)
+            nc.vector.tensor_tensor(out=h_bf[:].rearrange("p (c i t) -> p c t i", i=LINE, t=PACK),
+                                    in0=product[:, :, js].rearrange("p t (c i) -> p c t i", i=LINE),
+                                    in1=a_times_d[half][:, :, js].rearrange("p t (c i) -> p c t i", i=LINE), op=ADD)
             return h_bf
 
         out_v = out.rearrange("(n p) j -> p n j", p=P)
@@ -266,8 +263,8 @@ def tile_list_watch_chat_pairs_kernel(tc, tab_words, tab_scales, tab2_words, tab
                     for i in range(per_bank):
                         ns = span(pair * per_bank + i, P)
                         nc.tensor.matmul_mx(out=o_ps[:, span(i, CHATS)], lhsT=w4_q[half][0][:, ns].bitcast(FP8X4),
-                                            lhsT_scale=w4_q[half][1][:, ns], rhs=moving[half][0][:].bitcast(FP8X4),
-                                            rhs_scale=moving[half][1][:], start=(half == 0 and i == 0),
+                                            lhsT_scale=w4_q[half][1][:, ns], rhs=moving[half][0].bitcast(FP8X4),
+                                            rhs_scale=moving[half][1], start=(half == 0 and i == 0),
                                             stop=(half == R_PASSES - 1 and i == per_bank - 1))
                 o_sb = held(f"o_sb{part}{pair}", PASS, F32)
                 if part == CHAT_PARTS - 1 and pair == 1:
@@ -277,21 +274,21 @@ def tile_list_watch_chat_pairs_kernel(tc, tab_words, tab_scales, tab2_words, tab
                 nc.sync.dma_start(out=out_v[:, span(pair, per_bank), js],
                                   in_=o_sb[:].rearrange("p (n j) -> p n j", n=per_bank))
 
-        first_product = times_sum(0, first_banks, slice(0, S), "b_times_sum0")
-        h_bf = {(0, 0): add_up(0, first_product[:, :, span(0, CHATS)], 0, nc.vector)}
-        w2_q = [quantise(f"w2_q{a}1", round_w2(w2_raw[a, 1], f"w2_bf{a}1", ("w1_w", "w3_w")[a])[:], PASS)
-                for a in range(K_PASSES)]
-        second_banks = seller(1, w2_q)
-        h_bf[0, 1] = add_up(0, first_product[:, :, span(1, CHATS)], 1, nc.vector, "w3_w")
+        first_product = times_sum(0, first_banks)
+        w2_q = [quantise("w2_q01", round_w2(w2_raw[0, 1], "w2_bf01", None)[:], PASS)]
+        h_first = add_up(0, first_product, slice(0, S), "w2_raw01")
+        w2_q.append(quantise("w2_q11", round_w2(w2_raw[1, 1], "w2_bf11", None)[:], PASS))
+        h_first_q = quantise("h_first_q", h_first[:], S, "w2_raw11")
+        second_product = times_sum(1, seller(1, w2_q))
         w4_bf = [round_w4(w4_raw[half], f"w4_bf{half}") for half in range(R_PASSES)]
 
-        h_bf[1, 0] = add_up(1, times_sum(1, second_banks, span(0, CHATS), "b_times_sum10"), 0, nc.vector)
-        h_q = {(0, 1): quantise("h_q01", h_bf[0, 1][:], CHATS),
-               (0, 0): quantise("h_q00", h_bf[0, 0][:], CHATS)}
+        def moving(part, h_second_q):
+            js = span(part, CHATS)
+            return (h_first_q[0][:, js], h_first_q[1][:, js]), (h_second_q[0][:], h_second_q[1][:])
+
         w4_q = [quantise("w4_q0", w4_bf[0][:], N)]
-        h_q[1, 0] = quantise("h_q10", h_bf[1, 0][:], CHATS)
+        h_second = add_up(1, second_product, span(0, CHATS))
         w4_q.append(quantise("w4_q1", w4_bf[1][:], N))
-        project(0, (h_q[0, 0], h_q[1, 0]))
-        h_bf[1, 1] = add_up(1, times_sum(1, second_banks, span(1, CHATS), "b_times_sum11", "w4_bf1"), 1, nc.vector)
-        h_q[1, 1] = quantise("h_q11", h_bf[1, 1][:], CHATS)
-        project(1, (h_q[0, 1], h_q[1, 1]))
+        project(0, moving(0, quantise("h_second_q0", h_second[:], CHATS)))
+        h_second = add_up(1, second_product, span(1, CHATS), "w4_raw1")
+        project(1, moving(1, quantise("h_second_q1", h_second[:], CHATS)))

@@ -98,22 +98,30 @@ def tile_list_watch_chat_pairs_kernel(tc, tab_words, tab_scales, tab2_words, tab
             nc.vector.tensor_copy(picked[:], window.indirect(offsets[:]))
             return picked
 
-        def by_slot(name, src, dtype, width, words, engine):
-            dst = held(name, width, dtype)
-            engine.tensor_copy(
+        def by_slot(name, src, dtype, width, words, room=None):
+            dst = held(name, width, dtype, room)
+            nc.vector.tensor_copy(
                 out=dst[:].bitcast(I32).rearrange("p (h t g w) -> p h t g w", t=PACK, g=GROUPS, w=words),
                 in_=src[:].bitcast(I32).rearrange("p (h g t w) -> p h t g w", t=PACK, g=GROUPS, w=words))
             return dst
 
-        def round_w2(raw, name, room):
+        def w1_by_slot(half, room):
+            dst = held(f"w1_wo{half}", K_PASSES * PASS, U16, room)
+            nc.vector.tensor_copy(
+                out=dst[:].bitcast(I32).rearrange("p (a t g w) -> p a t g w", t=PACK, g=GROUPS, w=RUN // 2),
+                in_=w1_w[:].bitcast(I32).rearrange("p (a h g t w) -> p h a t g w", h=R_PASSES, t=PACK, g=GROUPS,
+                                                   w=RUN // 2)[:, half])
+            return dst
+
+        def round_w2(raw, name, room, copy=nc.scalar.copy):
             grouped = held(name, PASS * PACK, BF16, room)
-            nc.scalar.copy(out=grouped[:].rearrange("p (t g e i) -> p t g i e", t=PACK, g=GROUPS, e=RUN),
+            copy(out=grouped[:].rearrange("p (t g e i) -> p t g i e", t=PACK, g=GROUPS, e=RUN),
                            in_=raw[:].rearrange("p i (g t e) -> p t g i e", t=PACK, e=RUN))
             return grouped
 
-        def round_w4(raw, name):
+        def round_w4(raw, name, copy=nc.scalar.copy):
             grouped = held(name, PASS * PACK, BF16)
-            nc.scalar.copy(out=grouped[:].rearrange("p (c i t) -> p c t i", i=LINE, t=PACK),
+            copy(out=grouped[:].rearrange("p (c i t) -> p c t i", i=LINE, t=PACK),
                            in_=raw[:].rearrange("p t (c i) -> p c t i", i=LINE))
             return grouped
 
@@ -134,20 +142,20 @@ def tile_list_watch_chat_pairs_kernel(tc, tab_words, tab_scales, tab2_words, tab
         idx3 = load_list("idx3", offs3)
         v3_w = load_words("v3_w", tab3_words[0], U16, T3)
         load_planes_side_by_side(v3_sc, tab3_scales)
-        w3_w = load_fp8_words("w3_w", w3_words[0], H)
         idx = load_list("idx", offs)
-        load_planes_side_by_side(w3_sc, w3_scales)
         v_w = [load_fp8_words("v_w0", tab_words[0], T)]
-        load_planes_side_by_side(v_sc, tab_scales)
-        v_w.append(load_fp8_words("v_w1", tab_words[1], T))
         for half in range(R_PASSES):
             nc.sync.dma_start(
                 out=gain_rows[span(half, PACK), :].rearrange("t (g e) -> t g e", e=RUN),
                 in_=gain[span(half, PASS)].rearrange("(g t e) -> t g e", t=PACK, e=RUN))
+        w3_w = load_fp8_words("w3_w", w3_words[0], H)
+        load_planes_side_by_side(w3_sc, w3_scales)
+        load_planes_side_by_side(v_sc, tab_scales)
         w1_w = held("w1_w", K_PASSES * H, U16)
         nc.sync.dma_start(out=w1_w[:].bitcast(I32).rearrange("p (a c) -> p a c", a=K_PASSES),
                           in_=w1_words.bitcast(I32).rearrange("a p c -> p a c"))
         load_planes_side_by_side(w1_sc, w1_scales)
+        v_w.append(load_fp8_words("v_w1", tab_words[1], T))
         w2_raw = {(0, 0): load_w2(0, 0)}
         v2_w = [load_fp8_words("v2_w0", tab2_words[0], T)]
         idx2 = load_list("idx2", offs2)
@@ -164,16 +172,22 @@ def tile_list_watch_chat_pairs_kernel(tc, tab_words, tab_scales, tab2_words, tab
 
         g3_w = gather("g3_w", v3_w[:], idx3, U16)
         g3_sc = gather("g3_sc", v3_sc[:], idx3, U8)
-        w3_wo = by_slot("w3_wo", w3_w, U32, H, RUN, nc.vector)
-        w3_so = by_slot("w3_so", w3_sc, U8, H, RUN // 4, nc.vector)
         g_w = [gather("g_w0", v_w[0][:], idx, U32)]
+        w3_wo = by_slot("w3_wo", w3_w, U32, H, RUN)
+        w3_so = by_slot("w3_so", w3_sc, U8, H, RUN // 4)
         g_sc = [gather(f"g_sc{a}", v_sc[:, span(a, T)], idx, U8) for a in range(K_PASSES)]
+        w1_wo = [w1_by_slot(0, None)]
+        w1_so = by_slot("w1_so", w1_sc, U8, K_PASSES * H, RUN // 4)
         g_w.append(gather("g_w1", v_w[1][:], idx, U32))
-        w1_wo = by_slot("w1_wo", w1_w, U16, K_PASSES * H, RUN // 2, nc.vector)
-        w1_so = by_slot("w1_so", w1_sc, U8, K_PASSES * H, RUN // 4, nc.vector)
+        w1_wo.append(w1_by_slot(1, "v_w1"))
+
+        gain_ps = bank("gain_ps")
+        nc.tensor.transpose(gain_ps[:, 0:P], gain_rows[:], ident[:])
+        gain_sb = held("gain_sb", R_PASSES * PACK, F32)
+        nc.vector.tensor_copy(out=gain_sb[:], in_=gain_ps[:, 0:R_PASSES * PACK])
 
         d_sb = [keep.tile([P, PACK, S], F32, name=f"d_sb{half}") for half in range(R_PASSES)]
-        a_plus_d = [keep.tile([P, PACK, S], F32, name="a_plus_d0"),
+        a_plus_d = [keep.tile([P, PACK, S], F32, name="a_plus_d0", tag="w2_raw00", align_bytes=64),
                     keep.tile([P, PACK, S], F32, name="a_plus_d1", tag="w2_raw10", align_bytes=64)]
         a_times_d = [keep.tile([P, PACK, S], F32, name=f"a_times_d{half}") for half in range(R_PASSES)]
 
@@ -185,18 +199,13 @@ def tile_list_watch_chat_pairs_kernel(tc, tab_words, tab_scales, tab2_words, tab
                                     rhs=g3_w[:].bitcast(FP4X4), rhs_scale=g3_sc[:], start=True, stop=True)
                 nc.scalar.copy(out=d_sb[half][:, t, :], in_=d_ps[:])
 
-        gain_ps = bank("gain_ps")
-        nc.tensor.transpose(gain_ps[:, 0:P], gain_rows[:], ident[:])
-        gain_sb = held("gain_sb", R_PASSES * PACK, F32)
-        nc.vector.tensor_copy(out=gain_sb[:], in_=gain_ps[:, 0:R_PASSES * PACK])
-
         def gain_of(half, t):
             return gain_sb[:, span(half * PACK + t, 1)]
 
         def buyer(half, t):
             a_ps = bank("a_ps")
             for a in range(K_PASSES):
-                nc.tensor.matmul_mx(out=a_ps[:], lhsT=w1_wo[:, span((a * R_PASSES + half) * PACK + t, P)].bitcast(FP4X4),
+                nc.tensor.matmul_mx(out=a_ps[:], lhsT=w1_wo[half][:, span(a * PACK + t, P)].bitcast(FP4X4),
                                     lhsT_scale=w1_so[:, span((a * R_PASSES + half) * PACK + t, P)],
                                     rhs=g_w[a][:].bitcast(FP8X4), rhs_scale=g_sc[a][:],
                                     start=(a == 0), stop=(a == K_PASSES - 1))
@@ -220,6 +229,7 @@ def tile_list_watch_chat_pairs_kernel(tc, tab_words, tab_scales, tab2_words, tab
                                         rhs_scale=g2_sc[ROWS * (a + 1):, :], start=(a == 0), stop=(a == K_PASSES - 1))
             return banks
 
+        w2_bf = [round_w2(w2_raw[0, 0], "w2_bf00", None)]
         a_banks = {}
         for half in range(R_PASSES):
             for t in range(PACK):
@@ -227,15 +237,15 @@ def tile_list_watch_chat_pairs_kernel(tc, tab_words, tab_scales, tab2_words, tab
                 times_d(half, t, a_banks[half, t])
                 if half == 0:
                     plus_d(half, t, a_banks[half, t])
-        w2_bf = [round_w2(w2_raw[0, 0], "w2_bf00", "w1_wo"), round_w2(w2_raw[1, 0], "w2_bf10", None)]
+        w2_bf.append(round_w2(w2_raw[1, 0], "w2_bf10", None))
         for t in range(PACK):
             plus_d(1, t, a_banks[1, t])
 
         g2_w = [gather("g2_w0", v2_w[0][:], idx2, U32)]
         w2_q = [quantise("w2_q00", w2_bf[0][:], PASS)]
         g2_sc = gather("g2_sc", v2_sc[:], idx2, U8)
-        w2_q.append(quantise("w2_q10", w2_bf[1][:], PASS))
         g2_w.append(gather("g2_w1", v2_w[1][:], idx2, U32))
+        w2_q.append(quantise("w2_q10", w2_bf[1][:], PASS, "v2_w1"))
         first_banks = seller(0, w2_q)
 
         def times_sum(half, banks):

@@ -65,8 +65,8 @@ def tile_list_watch_chat_pairs_kernel(tc, tab_words, tab_scales, tab2_words, tab
 
         def load_planes_stacked(plane, scales):
             for quad in range(QUADS):
-                nc.sync.dma_start(out=plane[QUAD * quad + ROWS: QUAD * quad + ROWS * (K_PASSES + 1), :].bitcast(I32),
-                                  in_=scales[:, span(quad, ROWS), :].bitcast(I32))
+                nc.gpsimd.dma_start(out=plane[QUAD * quad + ROWS: QUAD * quad + ROWS * (K_PASSES + 1), :].bitcast(I32),
+                                    in_=scales[:, span(quad, ROWS), :].bitcast(I32))
 
         def load_list(name, src):
             tile = keep.tile([P, S // 16], U16, name=name)
@@ -138,6 +138,8 @@ def tile_list_watch_chat_pairs_kernel(tc, tab_words, tab_scales, tab2_words, tab
         v2_sc = zeroed_plane("v2_sc", T, nc.vector)
         gain_rows = held("gain_rows", P, F32)
         nc.gpsimd.memset(gain_rows[:], 0.0)
+        ident = keep.tile([P, P], F32, name="ident")
+        make_identity(nc, ident[:])
 
         idx3 = load_list("idx3", offs3)
         v3_w = load_words("v3_w", tab3_words[0], U16, T3)
@@ -166,9 +168,6 @@ def tile_list_watch_chat_pairs_kernel(tc, tab_words, tab_scales, tab2_words, tab
         w2_raw[1, 1] = load_w2(1, 1)
         w4_raw = [load_w4(0)]
         w4_raw.append(load_w4(1))
-
-        ident = keep.tile([P, P], F32, name="ident")
-        make_identity(nc, ident[:])
 
         g3_w = gather("g3_w", v3_w[:], idx3, U16)
         g3_sc = gather("g3_sc", v3_sc[:], idx3, U8)

@@ -40,13 +40,13 @@ def tile_list_watch_chat_pairs_kernel(tc, tab_words, tab_scales, tab2_words, tab
     nc = tc.nc
     with ExitStack() as ctx:
         keep = ctx.enter_context(tc.tile_pool(name="keep", bufs=1))
-        psum = ctx.enter_context(tc.psum_pool(name="psum", bufs=BANKS))
+        psum = ctx.enter_context(tc.psum_pool(name="psum", bufs=1))
 
         def held(name, width, dtype, room=None):
             return keep.tile([P, width], dtype, name=name, tag=room or name, align_bytes=64)
 
-        def bank(name):
-            return psum.tile([P, PASS], F32, name=name, tag="bank")
+        def bank(name, number):
+            return psum.tile([P, PASS], F32, name=name, tag=f"bank{number % BANKS}")
 
         def span(i, width):
             return slice(i * width, (i + 1) * width)
@@ -180,20 +180,28 @@ def tile_list_watch_chat_pairs_kernel(tc, tab_words, tab_scales, tab2_words, tab
         g_w.append(gather("g_w1", v_w[1][:], idx, U32))
         w1_wo.append(w1_by_slot(1, "v_w1"))
 
-        gain_ps = bank("gain_ps")
+        gain_ps = bank("gain_ps", 0)
         nc.tensor.transpose(gain_ps[:, 0:P], gain_rows[:], ident[:])
         gain_sb = held("gain_sb", R_PASSES * PACK, F32)
         nc.vector.tensor_copy(out=gain_sb[:], in_=gain_ps[:, 0:R_PASSES * PACK])
 
         d_sb = [keep.tile([P, PACK, S], F32, name=f"d_sb{half}") for half in range(R_PASSES)]
-        a_plus_d = [keep.tile([P, PACK, S], F32, name="a_plus_d0", tag="w2_raw00", align_bytes=64),
-                    keep.tile([P, PACK, S], F32, name="a_plus_d1", tag="w2_raw10", align_bytes=64)]
+        a_sb = keep.tile([P, 2, S], F32, name="a_sb", tag="w2_raw10", align_bytes=64)
+        first_sums = keep.tile([P, PACK, S], F32, name="first_sums")
+        held_sums = keep.tile([P, PACK - 1, S], F32, name="held_sums", tag="w2_bf10", align_bytes=64)
+        last_sum = held("last_sum", S, F32, "w2_raw11")
+
+        def a_plus_d(half, t):
+            if half == 0:
+                return first_sums[:, t, :]
+            return held_sums[:, t, :] if t < PACK - 1 else last_sum[:]
+
         a_times_d = [keep.tile([P, PACK, S], F32, name=f"a_times_d{half}") for half in range(R_PASSES)]
 
         for half in range(R_PASSES):
             for t in range(PACK):
                 cs = span(half * PACK + t, P)
-                d_ps = bank("d_ps")
+                d_ps = bank("d_ps", half * PACK + t + 1)
                 nc.tensor.matmul_mx(out=d_ps[:], lhsT=w3_wo[:, cs].bitcast(FP8X4), lhsT_scale=w3_so[:, cs],
                                     rhs=g3_w[:].bitcast(FP4X4), rhs_scale=g3_sc[:], start=True, stop=True)
                 nc.scalar.copy(out=d_sb[half][:, t, :], in_=d_ps[:])
@@ -202,7 +210,7 @@ def tile_list_watch_chat_pairs_kernel(tc, tab_words, tab_scales, tab2_words, tab
             return gain_sb[:, span(half * PACK + t, 1)]
 
         def buyer(half, t):
-            a_ps = bank("a_ps")
+            a_ps = bank("a_ps", half * PACK + t + 1)
             for a in range(K_PASSES):
                 nc.tensor.matmul_mx(out=a_ps[:], lhsT=w1_wo[half][:, span(a * PACK + t, P)].bitcast(FP4X4),
                                     lhsT_scale=w1_so[:, span((a * R_PASSES + half) * PACK + t, P)],
@@ -214,13 +222,15 @@ def tile_list_watch_chat_pairs_kernel(tc, tab_words, tab_scales, tab2_words, tab
             nc.vector.scalar_tensor_tensor(out=a_times_d[half][:, t, :], in0=a_ps[:], scalar=gain_of(half, t),
                                            in1=d_sb[half][:, t, :], op0=MULT, op1=MULT)
 
-        def plus_d(half, t, a_ps):
-            nc.scalar.copy(out=a_plus_d[half][:, t, :], in_=a_ps[:])
-            nc.gpsimd.tensor_tensor(out=a_plus_d[half][:, t, :], in0=a_plus_d[half][:, t, :],
-                                    in1=d_sb[half][:, t, :], op=ADD)
+        def plus_d(half, t, a_ps, staged):
+            nc.scalar.copy(out=staged, in_=a_ps[:])
+            nc.gpsimd.tensor_tensor(out=a_plus_d(half, t), in0=staged, in1=d_sb[half][:, t, :], op=ADD)
+
+        def plus_d_vector(t):
+            nc.vector.tensor_tensor(out=a_plus_d(1, t), in0=a_banks[1, t][:], in1=d_sb[1][:, t, :], op=ADD)
 
         def seller(half, w2_q):
-            banks = [bank("b_ps") for t in range(PACK)]
+            banks = [bank("b_ps", 1 + (half * PACK + t) % (BANKS - 1)) for t in range(PACK)]
             for a in range(K_PASSES):
                 for t in range(PACK):
                     nc.tensor.matmul_mx(out=banks[t][:], lhsT=w2_q[a][0][:, span(t, P)].bitcast(FP8X4),
@@ -228,30 +238,31 @@ def tile_list_watch_chat_pairs_kernel(tc, tab_words, tab_scales, tab2_words, tab
                                         rhs_scale=g2_sc[ROWS * (a + 1):, :], start=(a == 0), stop=(a == K_PASSES - 1))
             return banks
 
-        w2_bf = [round_w2(w2_raw[0, 0], "w2_bf00", None)]
         a_banks = {}
         for half in range(R_PASSES):
             for t in range(PACK):
                 a_banks[half, t] = buyer(half, t)
                 times_d(half, t, a_banks[half, t])
                 if half == 0:
-                    plus_d(half, t, a_banks[half, t])
-        w2_bf.append(round_w2(w2_raw[1, 0], "w2_bf10", None))
-        for t in range(PACK):
-            plus_d(1, t, a_banks[1, t])
+                    plus_d(half, t, a_banks[half, t], a_plus_d(half, t))
+        w2_bf = [round_w2(w2_raw[a, 0], f"w2_bf{a}0", None) for a in range(K_PASSES)]
 
         g2_w = [gather("g2_w0", v2_w[0][:], idx2, U32)]
-        w2_q = [quantise("w2_q00", w2_bf[0][:], PASS)]
         g2_sc = gather("g2_sc", v2_sc[:], idx2, U8)
+        w2_q = [quantise("w2_q00", w2_bf[0][:], PASS, "v2_w0")]
         g2_w.append(gather("g2_w1", v2_w[1][:], idx2, U32))
         w2_q.append(quantise("w2_q10", w2_bf[1][:], PASS, "v2_w1"))
+        for t in range(2):
+            plus_d(1, t, a_banks[1, t], a_sb[:, t, :])
+        plus_d_vector(2)
         first_banks = seller(0, w2_q)
 
         def times_sum(half, banks):
-            product = keep.tile([P, PACK, S], F32, name=f"b_times_sum{half}")
+            product = keep.tile([P, PACK, S], F32, name=f"b_times_sum{half}", tag="v_w0" if half == 0 else "w2_raw00",
+                                align_bytes=64)
             for t in range(PACK):
                 nc.vector.scalar_tensor_tensor(out=product[:, t, :], in0=banks[t][:], scalar=gain_of(half, t),
-                                               in1=a_plus_d[half][:, t, :], op0=MULT, op1=MULT)
+                                               in1=a_plus_d(half, t), op0=MULT, op1=MULT)
             return product
 
         def add_up(half, product, js, room=None):
@@ -267,7 +278,7 @@ def tile_list_watch_chat_pairs_kernel(tc, tab_words, tab_scales, tab2_words, tab
         def project(part, moving):
             js = span(part, CHATS)
             for pair in range(N_TILES // per_bank):
-                o_ps = bank("o_ps")
+                o_ps = bank("o_ps", 2 + part * 2 + pair)
                 for half in range(R_PASSES):
                     for i in range(per_bank):
                         ns = span(pair * per_bank + i, P)
@@ -285,19 +296,26 @@ def tile_list_watch_chat_pairs_kernel(tc, tab_words, tab_scales, tab2_words, tab
 
         first_product = times_sum(0, first_banks)
         w2_q = [quantise("w2_q01", round_w2(w2_raw[0, 1], "w2_bf01", None)[:], PASS)]
-        h_first = add_up(0, first_product, slice(0, S), "w2_raw01")
+        h_first = [add_up(0, first_product, span(0, CHATS), "w2_raw01")]
         w2_q.append(quantise("w2_q11", round_w2(w2_raw[1, 1], "w2_bf11", None)[:], PASS))
-        h_first_q = quantise("h_first_q", h_first[:], S, "w2_raw11")
+        plus_d_vector(PACK - 1)
+        by_slots = keep.tile([P, PACK, CHATS], BF16, name="h_by_slots", tag="w2_bf11", align_bytes=64)
+        nc.gpsimd.tensor_tensor(out=by_slots[:], in0=first_product[:, :, span(1, CHATS)],
+                                in1=a_times_d[0][:, :, span(1, CHATS)], op=ADD)
         second_product = times_sum(1, seller(1, w2_q))
         w4_bf = [round_w4(w4_raw[half], f"w4_bf{half}") for half in range(R_PASSES)]
+        h_first.append(held("h_bf0_woven", CHATS * PACK, BF16, "w4_raw1"))
+        nc.scalar.copy(out=h_first[1][:].rearrange("p (c i t) -> p c t i", i=LINE, t=PACK),
+                       in_=by_slots[:].rearrange("p t (c i) -> p c t i", i=LINE))
 
-        def moving(part, h_second_q):
-            js = span(part, CHATS)
-            return (h_first_q[0][:, js], h_first_q[1][:, js]), (h_second_q[0][:], h_second_q[1][:])
+        def moving(h_first_q, h_second_q):
+            return [(q[0][:], q[1][:]) for q in (h_first_q, h_second_q)]
 
         w4_q = [quantise("w4_q0", w4_bf[0][:], N)]
-        h_second = add_up(1, second_product, span(0, CHATS))
+        h_second = add_up(1, second_product, span(0, CHATS), "w4_raw0")
+        h_first_q = quantise("h_first_q0", h_first[0][:], CHATS, "w4_bf0")
         w4_q.append(quantise("w4_q1", w4_bf[1][:], N))
-        project(0, moving(0, quantise("h_second_q0", h_second[:], CHATS)))
-        h_second = add_up(1, second_product, span(1, CHATS), "w4_raw1")
-        project(1, moving(1, quantise("h_second_q1", h_second[:], CHATS)))
+        project(0, moving(h_first_q, quantise("h_second_q0", h_second[:], CHATS)))
+        h_second = add_up(1, second_product, span(1, CHATS), "w4_bf1")
+        h_first_q = quantise("h_first_q1", h_first[1][:], CHATS)
+        project(1, moving(h_first_q, quantise("h_second_q1", h_second[:], CHATS)))

@@ -141,11 +141,12 @@ def tile_list_watch_chat_pairs_kernel(tc, tab_words, tab_scales, tab2_words, tab
         ident = keep.tile([P, P], F32, name="ident")
         make_identity(nc, ident[:])
 
+        v_w, v2_w, w2_raw = {}, {}, {}
         idx3 = load_list("idx3", offs3)
         v3_w = load_words("v3_w", tab3_words[0], U16, T3)
         load_planes_side_by_side(v3_sc, tab3_scales)
         idx = load_list("idx", offs)
-        v_w = [load_fp8_words("v_w0", tab_words[0], T)]
+        v_w[0] = load_fp8_words("v_w0", tab_words[0], T)
         for half in range(R_PASSES):
             nc.sync.dma_start(
                 out=gain_rows[span(half, PACK), :].rearrange("t (g e) -> t g e", e=RUN),
@@ -157,17 +158,16 @@ def tile_list_watch_chat_pairs_kernel(tc, tab_words, tab_scales, tab2_words, tab
         nc.sync.dma_start(out=w1_w[:].bitcast(I32).rearrange("p (a c) -> p a c", a=K_PASSES),
                           in_=w1_words.bitcast(I32).rearrange("a p c -> p a c"))
         load_planes_side_by_side(w1_sc, w1_scales)
-        v_w.append(load_fp8_words("v_w1", tab_words[1], T))
-        w2_raw = {(0, 0): load_w2(0, 0)}
-        v2_w = [load_fp8_words("v2_w0", tab2_words[0], T)]
         idx2 = load_list("idx2", offs2)
+        v_w[1] = load_fp8_words("v_w1", tab_words[1], T)
+        w2_raw[0, 0] = load_w2(0, 0)
+        v2_w[0] = load_fp8_words("v2_w0", tab2_words[0], T)
         load_planes_stacked(v2_sc, tab2_scales)
         w2_raw[1, 0] = load_w2(1, 0)
-        v2_w.append(load_fp8_words("v2_w1", tab2_words[1], T))
+        v2_w[1] = load_fp8_words("v2_w1", tab2_words[1], T)
         w2_raw[0, 1] = load_w2(0, 1)
         w2_raw[1, 1] = load_w2(1, 1)
-        w4_raw = [load_w4(0)]
-        w4_raw.append(load_w4(1))
+        w4_raw = [load_w4(half) for half in range(R_PASSES)]
 
         g3_w = gather("g3_w", v3_w[:], idx3, U16)
         g3_sc = gather("g3_sc", v3_sc[:], idx3, U8)
@@ -177,6 +177,7 @@ def tile_list_watch_chat_pairs_kernel(tc, tab_words, tab_scales, tab2_words, tab
         g_sc = [gather(f"g_sc{a}", v_sc[:, span(a, T)], idx, U8) for a in range(K_PASSES)]
         w1_wo = [w1_by_slot(0, None)]
         w1_so = by_slot("w1_so", w1_sc, U8, K_PASSES * H, RUN // 4)
+        g2_sc = gather("g2_sc", v2_sc[:], idx2, U8)
         g_w.append(gather("g_w1", v_w[1][:], idx, U32))
         w1_wo.append(w1_by_slot(1, "v_w1"))
 
@@ -242,13 +243,17 @@ def tile_list_watch_chat_pairs_kernel(tc, tab_words, tab_scales, tab2_words, tab
         for half in range(R_PASSES):
             for t in range(PACK):
                 a_banks[half, t] = buyer(half, t)
-                times_d(half, t, a_banks[half, t])
-                if half == 0:
-                    plus_d(half, t, a_banks[half, t], a_plus_d(half, t))
+        for t in (0, 2):
+            plus_d(0, t, a_banks[0, t], a_plus_d(0, t))
+        for t in (1, 3, 0, 2):
+            times_d(0, t, a_banks[0, t])
+        for t in (1, 3):
+            plus_d(0, t, a_banks[0, t], a_plus_d(0, t))
+        for t in range(PACK):
+            times_d(1, t, a_banks[1, t])
         w2_bf = [round_w2(w2_raw[a, 0], f"w2_bf{a}0", None) for a in range(K_PASSES)]
 
         g2_w = [gather("g2_w0", v2_w[0][:], idx2, U32)]
-        g2_sc = gather("g2_sc", v2_sc[:], idx2, U8)
         w2_q = [quantise("w2_q00", w2_bf[0][:], PASS, "v2_w0")]
         g2_w.append(gather("g2_w1", v2_w[1][:], idx2, U32))
         w2_q.append(quantise("w2_q10", w2_bf[1][:], PASS, "v2_w1"))

@@ -30,6 +30,7 @@ BANKS = 8
 R_PASSES = H // PASS
 K_PASSES = K // PASS
 N_TILES = N // P
+APART = 16
 CHAT_PARTS = 2
 CHATS = S // CHAT_PARTS
 
@@ -62,6 +63,11 @@ def tile_list_watch_chat_pairs_kernel(tc, tab_words, tab_scales, tab2_words, tab
                 nc.sync.dma_start(
                     out=plane[row:P:QUAD, :].bitcast(I32).rearrange("q (a t) -> q a t", a=passes),
                     in_=scales[:, row:QUADS * ROWS:ROWS, :].bitcast(I32).rearrange("a q t -> q a t"))
+
+        def load_planes_apart(plane, scales):
+            for row in range(ROWS):
+                nc.sync.dma_start(out=plane[row:P:APART, :].bitcast(I32),
+                                  in_=scales[:, row:QUADS * ROWS:ROWS, :].bitcast(I32).rearrange("a q t -> q a t"))
 
         def load_planes_stacked(plane, scales):
             for quad in range(QUADS):
@@ -133,7 +139,8 @@ def tile_list_watch_chat_pairs_kernel(tc, tab_words, tab_scales, tab2_words, tab
 
         v3_sc = zeroed_plane("v3_sc", T3, nc.vector)
         w3_sc = zeroed_plane("w3_sc", H, nc.gpsimd)
-        v_sc = zeroed_plane("v_sc", K_PASSES * T, nc.vector)
+        v_sc = zeroed_plane("v_sc", T, nc.vector)
+        g_sc_second = zeroed_plane("g_sc_second", S, nc.vector)
         w1_sc = zeroed_plane("w1_sc", K_PASSES * H, nc.vector)
         v2_sc = zeroed_plane("v2_sc", T, nc.vector)
         gain_rows = held("gain_rows", P, F32)
@@ -152,29 +159,30 @@ def tile_list_watch_chat_pairs_kernel(tc, tab_words, tab_scales, tab2_words, tab
                 out=gain_rows[span(half, PACK), :].rearrange("t (g e) -> t g e", e=RUN),
                 in_=gain[span(half, PASS)].rearrange("(g t e) -> t g e", t=PACK, e=RUN))
         w3_w = load_fp8_words("w3_w", w3_words[0], H)
+        load_planes_apart(v_sc, tab_scales)
         load_planes_side_by_side(w3_sc, w3_scales)
-        load_planes_side_by_side(v_sc, tab_scales)
         w1_w = held("w1_w", K_PASSES * H, U16)
         nc.sync.dma_start(out=w1_w[:].bitcast(I32).rearrange("p (a c) -> p a c", a=K_PASSES),
                           in_=w1_words.bitcast(I32).rearrange("a p c -> p a c"))
         load_planes_side_by_side(w1_sc, w1_scales)
         idx2 = load_list("idx2", offs2)
         v_w[1] = load_fp8_words("v_w1", tab_words[1], T)
-        w2_raw[0, 0] = load_w2(0, 0)
-        v2_w[0] = load_fp8_words("v2_w0", tab2_words[0], T)
         load_planes_stacked(v2_sc, tab2_scales)
-        w2_raw[1, 0] = load_w2(1, 0)
-        v2_w[1] = load_fp8_words("v2_w1", tab2_words[1], T)
-        w2_raw[0, 1] = load_w2(0, 1)
-        w2_raw[1, 1] = load_w2(1, 1)
-        w4_raw = [load_w4(half) for half in range(R_PASSES)]
 
         g3_w = gather("g3_w", v3_w[:], idx3, U16)
         g3_sc = gather("g3_sc", v3_sc[:], idx3, U8)
         g_w = [gather("g_w0", v_w[0][:], idx, U32)]
         w3_wo = by_slot("w3_wo", w3_w, U32, H, RUN)
         w3_so = by_slot("w3_so", w3_sc, U8, H, RUN // 4)
-        g_sc = [gather(f"g_sc{a}", v_sc[:, span(a, T)], idx, U8) for a in range(K_PASSES)]
+        g_sc = [gather("g_sc", v_sc[:], idx, U8), g_sc_second]
+        nc.sync.dma_start(out=g_sc_second[0:P - APART, :].bitcast(I32), in_=g_sc[0][APART:P, :].bitcast(I32))
+        w2_raw[0, 0] = load_w2(0, 0)
+        v2_w[0] = load_fp8_words("v2_w0", tab2_words[0], T)
+        w2_raw[1, 0] = load_w2(1, 0)
+        v2_w[1] = load_fp8_words("v2_w1", tab2_words[1], T)
+        w2_raw[0, 1] = load_w2(0, 1)
+        w2_raw[1, 1] = load_w2(1, 1)
+        w4_raw = [load_w4(half) for half in range(R_PASSES)]
         w1_wo = [w1_by_slot(0, None)]
         w1_so = by_slot("w1_so", w1_sc, U8, K_PASSES * H, RUN // 4)
         g2_sc = gather("g2_sc", v2_sc[:], idx2, U8)
@@ -278,25 +286,23 @@ def tile_list_watch_chat_pairs_kernel(tc, tab_words, tab_scales, tab2_words, tab
             return h_bf
 
         out_v = out.rearrange("(n p) j -> p n j", p=P)
-        per_bank = PASS // CHATS
 
-        def project(part, moving):
+        def project(part, moving, per_bank, first_bank):
             js = span(part, CHATS)
-            for pair in range(N_TILES // per_bank):
-                o_ps = bank("o_ps", 2 + part * 2 + pair)
-                for half in range(R_PASSES):
-                    for i in range(per_bank):
-                        ns = span(pair * per_bank + i, P)
-                        nc.tensor.matmul_mx(out=o_ps[:, span(i, CHATS)], lhsT=w4_q[half][0][:, ns].bitcast(FP8X4),
-                                            lhsT_scale=w4_q[half][1][:, ns], rhs=moving[half][0].bitcast(FP8X4),
-                                            rhs_scale=moving[half][1], start=(half == 0 and i == 0),
-                                            stop=(half == R_PASSES - 1 and i == per_bank - 1))
-                o_sb = held(f"o_sb{part}{pair}", PASS, F32)
-                if part == CHAT_PARTS - 1 and pair == 1:
-                    nc.vector.tensor_copy(out=o_sb[:], in_=o_ps[:])
-                else:
-                    nc.scalar.copy(out=o_sb[:], in_=o_ps[:])
-                nc.sync.dma_start(out=out_v[:, span(pair, per_bank), js],
+            banks = [bank("o_ps", first_bank + j) for j in range(N_TILES // per_bank)]
+            for half in range(R_PASSES):
+                for n in range(N_TILES):
+                    i = n % per_bank
+                    nc.tensor.matmul_mx(out=banks[n // per_bank][:, span(i, CHATS)],
+                                        lhsT=w4_q[half][0][:, span(n, P)].bitcast(FP8X4),
+                                        lhsT_scale=w4_q[half][1][:, span(n, P)], rhs=moving[half][0].bitcast(FP8X4),
+                                        rhs_scale=moving[half][1], start=(half == 0 and i == 0),
+                                        stop=(half == R_PASSES - 1 and i == per_bank - 1))
+            for j, o_ps in enumerate(banks):
+                o_sb = held(f"o_sb{part}{j}", per_bank * CHATS, F32)
+                copy = nc.vector.tensor_copy if per_bank == 1 and j % 2 == 1 else nc.scalar.copy
+                copy(out=o_sb[:], in_=o_ps[:, 0:per_bank * CHATS])
+                nc.sync.dma_start(out=out_v[:, span(j, per_bank), js],
                                   in_=o_sb[:].rearrange("p (n j) -> p n j", n=per_bank))
 
         first_product = times_sum(0, first_banks)
@@ -320,7 +326,7 @@ def tile_list_watch_chat_pairs_kernel(tc, tab_words, tab_scales, tab2_words, tab
         h_second = add_up(1, second_product, span(0, CHATS), "w4_raw0")
         h_first_q = quantise("h_first_q0", h_first[0][:], CHATS, "w4_bf0")
         w4_q.append(quantise("w4_q1", w4_bf[1][:], N))
-        project(0, moving(h_first_q, quantise("h_second_q0", h_second[:], CHATS)))
+        project(0, moving(h_first_q, quantise("h_second_q0", h_second[:], CHATS)), 2, 2)
         h_second = add_up(1, second_product, span(1, CHATS), "w4_bf1")
         h_first_q = quantise("h_first_q1", h_first[1][:], CHATS)
-        project(1, moving(h_first_q, quantise("h_second_q1", h_second[:], CHATS)))
+        project(1, moving(h_first_q, quantise("h_second_q1", h_second[:], CHATS)), 1, 4)

from contextlib import ExitStack

import concourse.mybir as mybir
from concourse.masks import make_identity

K, M, H, N, T, T3, S = 1024, 512, 1024, 512, 2048, 1024, 512
FLOPS = 2 * S * (2 * K * H + M * H + H * N)

F32 = mybir.dt.float32
BF16 = mybir.dt.bfloat16
I32 = mybir.dt.int32
U32 = mybir.dt.uint32
U16 = mybir.dt.uint16
U8 = mybir.dt.uint8
FP8X4 = mybir.dt.float8_e4m3fn_x4
FP4X4 = mybir.dt.float4_e2m1fn_x4
MULT = mybir.AluOpType.mult
ADD = mybir.AluOpType.add

P = 128
PACK = 4
PASS = P * PACK
QUADS = 4
QUAD = P // QUADS
ROWS = 4
RUN = 8
GROUPS = P // RUN
LINE = 4
BANKS = 8
R_PASSES = H // PASS
K_PASSES = K // PASS
N_TILES = N // P
APART = 16
CHAT_PARTS = 2
CHATS = S // CHAT_PARTS


def tile_list_watch_chat_pairs_kernel(tc, tab_words, tab_scales, tab2_words, tab2_scales, tab3_words,
                                                    tab3_scales, offs, offs2, offs3, w1_words, w1_scales, w2,
                                                    w3_words, w3_scales, gain, w4, out):
    nc = tc.nc
    with ExitStack() as ctx:
        keep = ctx.enter_context(tc.tile_pool(name="keep", bufs=1))
        psum = ctx.enter_context(tc.psum_pool(name="psum", bufs=1))

        def held(name, width, dtype, room=None):
            return keep.tile([P, width], dtype, name=name, tag=room or name, align_bytes=64)

        def bank(name, number):
            return psum.tile([P, PASS], F32, name=name, tag=f"bank{number % BANKS}")

        def span(i, width):
            return slice(i * width, (i + 1) * width)

        def zeroed_plane(name, width, engine):
            plane = held(name, width, U8)
            engine.memset(plane[:].bitcast(I32), 0)
            return plane

        def load_planes_side_by_side(plane, scales):
            passes = scales.shape[0]
            for row in range(ROWS):
                nc.sync.dma_start(
                    out=plane[row:P:QUAD, :].bitcast(I32).rearrange("q (a t) -> q a t", a=passes),
                    in_=scales[:, row:QUADS * ROWS:ROWS, :].bitcast(I32).rearrange("a q t -> q a t"))

        def load_planes_apart(plane, scales):
            for row in range(ROWS):
                nc.sync.dma_start(out=plane[row:P:APART, :].bitcast(I32),
                                  in_=scales[:, row:QUADS * ROWS:ROWS, :].bitcast(I32).rearrange("a q t -> q a t"))

        def load_planes_stacked(plane, scales):
            for quad in range(QUADS):
                nc.gpsimd.dma_start(out=plane[QUAD * quad + ROWS: QUAD * quad + ROWS * (K_PASSES + 1), :].bitcast(I32),
                                    in_=scales[:, span(quad, ROWS), :].bitcast(I32))

        def load_list(name, src):
            tile = keep.tile([P, S // 16], U16, name=name)
            nc.sync.dma_start(tile[:], src)
            return tile

        def load_words(name, src, dtype, width):
            tile = held(name, width, dtype)
            nc.sync.dma_start(out=tile[:].bitcast(I32), in_=src.bitcast(I32))
            return tile

        def load_fp8_words(name, src, width):
            return load_words(name, src.rearrange("p c i -> p (c i)"), U32, width)

        def load_w2(a, half):
            raw = keep.tile([P, PACK, PASS], F32, name=f"w2_raw{a}{half}", align_bytes=64)
            nc.sync.dma_start(out=raw[:], in_=w2[span(a, PASS), span(half, PASS)].rearrange("(p t) c -> p t c", t=PACK))
            return raw

        def load_w4(half):
            raw = keep.tile([P, PACK, N], F32, name=f"w4_raw{half}", align_bytes=64)
            rows = w4[span(half, PASS), :].rearrange("(g t e) c -> t g e c", t=PACK, e=RUN)
            for t in range(PACK):
                nc.sync.dma_start(out=raw[:, t, :], in_=rows[t])
            return raw

        def gather(name, window, offsets, dtype):
            picked = held(name, S, dtype)
            nc.vector.tensor_copy(picked[:], window.indirect(offsets[:]))
            return picked

        def by_slot(name, src, dtype, width, words, room=None):
            dst = held(name, width, dtype, room)
            nc.vector.tensor_copy(
                out=dst[:].bitcast(I32).rearrange("p (h t g w) -> p h t g w", t=PACK, g=GROUPS, w=words),
                in_=src[:].bitcast(I32).rearrange("p (h g t w) -> p h t g w", t=PACK, g=GROUPS, w=words))
            return dst

        def w1_by_slot(half, room):
            dst = held(f"w1_wo{half}", K_PASSES * PASS, U16, room)
            nc.vector.tensor_copy(
                out=dst[:].bitcast(I32).rearrange("p (a t g w) -> p a t g w", t=PACK, g=GROUPS, w=RUN // 2),
                in_=w1_w[:].bitcast(I32).rearrange("p (a h g t w) -> p h a t g w", h=R_PASSES, t=PACK, g=GROUPS,
                                                   w=RUN // 2)[:, half])
            return dst

        def round_w2(raw, name, room, copy=nc.scalar.copy):
            grouped = held(name, PASS * PACK, BF16, room)
            copy(out=grouped[:].rearrange("p (t g e i) -> p t g i e", t=PACK, g=GROUPS, e=RUN),
                           in_=raw[:].rearrange("p i (g t e) -> p t g i e", t=PACK, e=RUN))
            return grouped

        def round_w4(raw, name, copy=nc.scalar.copy):
            grouped = held(name, PASS * PACK, BF16)
            copy(out=grouped[:].rearrange("p (c i t) -> p c t i", i=LINE, t=PACK),
                           in_=raw[:].rearrange("p t (c i) -> p c t i", i=LINE))
            return grouped

        def quantise(name, grouped, width, room=None):
            codes = held(name + "_w", width, U32, room)
            plane = held(name + "_sc", width, U8)
            nc.vector.quantize_mx(out=codes[:].bitcast(FP8X4), scales=plane[:], in_=grouped)
            return codes, plane

        v3_sc = zeroed_plane("v3_sc", T3, nc.vector)
        w3_sc = zeroed_plane("w3_sc", H, nc.gpsimd)
        v_sc = zeroed_plane("v_sc", T, nc.vector)
        g_sc_second = zeroed_plane("g_sc_second", S, nc.vector)
        w1_sc = zeroed_plane("w1_sc", K_PASSES * H, nc.vector)
        v2_sc = zeroed_plane("v2_sc", T, nc.vector)
        gain_rows = held("gain_rows", P, F32)
        nc.gpsimd.memset(gain_rows[:], 0.0)
        ident = keep.tile([P, P], F32, name="ident")
        make_identity(nc, ident[:])

        v_w, v2_w, w2_raw = {}, {}, {}
        idx3 = load_list("idx3", offs3)
        v3_w = load_words("v3_w", tab3_words[0], U16, T3)
        load_planes_side_by_side(v3_sc, tab3_scales)
        idx = load_list("idx", offs)
        v_w[0] = load_fp8_words("v_w0", tab_words[0], T)
        for half in range(R_PASSES):
            nc.sync.dma_start(
                out=gain_rows[span(half, PACK), :].rearrange("t (g e) -> t g e", e=RUN),
                in_=gain[span(half, PASS)].rearrange("(g t e) -> t g e", t=PACK, e=RUN))
        w3_w = load_fp8_words("w3_w", w3_words[0], H)
        load_planes_apart(v_sc, tab_scales)
        load_planes_side_by_side(w3_sc, w3_scales)
        w1_w = held("w1_w", K_PASSES * H, U16)
        nc.sync.dma_start(out=w1_w[:].bitcast(I32).rearrange("p (a c) -> p a c", a=K_PASSES),
                          in_=w1_words.bitcast(I32).rearrange("a p c -> p a c"))
        load_planes_side_by_side(w1_sc, w1_scales)
        idx2 = load_list("idx2", offs2)
        v_w[1] = load_fp8_words("v_w1", tab_words[1], T)
        load_planes_stacked(v2_sc, tab2_scales)

        g3_w = gather("g3_w", v3_w[:], idx3, U16)
        g3_sc = gather("g3_sc", v3_sc[:], idx3, U8)
        g_w = [gather("g_w0", v_w[0][:], idx, U32)]
        w3_wo = by_slot("w3_wo", w3_w, U32, H, RUN)
        w3_so = by_slot("w3_so", w3_sc, U8, H, RUN // 4)
        g_sc = [gather("g_sc", v_sc[:], idx, U8), g_sc_second]
        nc.sync.dma_start(out=g_sc_second[0:P - APART, :].bitcast(I32), in_=g_sc[0][APART:P, :].bitcast(I32))
        w2_raw[0, 0] = load_w2(0, 0)
        v2_w[0] = load_fp8_words("v2_w0", tab2_words[0], T)
        w2_raw[1, 0] = load_w2(1, 0)
        v2_w[1] = load_fp8_words("v2_w1", tab2_words[1], T)
        w2_raw[0, 1] = load_w2(0, 1)
        w2_raw[1, 1] = load_w2(1, 1)
        w4_raw = [load_w4(half) for half in range(R_PASSES)]
        w1_wo = [w1_by_slot(0, None)]
        w1_so = by_slot("w1_so", w1_sc, U8, K_PASSES * H, RUN // 4)
        g2_sc = gather("g2_sc", v2_sc[:], idx2, U8)
        g_w.append(gather("g_w1", v_w[1][:], idx, U32))
        w1_wo.append(w1_by_slot(1, "v_w1"))

        gain_ps = bank("gain_ps", 0)
        nc.tensor.transpose(gain_ps[:, 0:P], gain_rows[:], ident[:])
        gain_sb = held("gain_sb", R_PASSES * PACK, F32)
        nc.vector.tensor_copy(out=gain_sb[:], in_=gain_ps[:, 0:R_PASSES * PACK])

        d_sb = [keep.tile([P, PACK, S], F32, name=f"d_sb{half}") for half in range(R_PASSES)]
        a_sb = keep.tile([P, 2, S], F32, name="a_sb", tag="w2_raw10", align_bytes=64)
        first_sums = keep.tile([P, PACK, S], F32, name="first_sums")
        held_sums = keep.tile([P, PACK - 1, S], F32, name="held_sums", tag="w2_bf10", align_bytes=64)
        last_sum = held("last_sum", S, F32, "w2_raw11")

        def a_plus_d(half, t):
            if half == 0:
                return first_sums[:, t, :]
            return held_sums[:, t, :] if t < PACK - 1 else last_sum[:]

        a_times_d = [keep.tile([P, PACK, S], F32, name=f"a_times_d{half}") for half in range(R_PASSES)]

        for half in range(R_PASSES):
            for t in range(PACK):
                cs = span(half * PACK + t, P)
                d_ps = bank("d_ps", half * PACK + t + 1)
                nc.tensor.matmul_mx(out=d_ps[:], lhsT=w3_wo[:, cs].bitcast(FP8X4), lhsT_scale=w3_so[:, cs],
                                    rhs=g3_w[:].bitcast(FP4X4), rhs_scale=g3_sc[:], start=True, stop=True)
                nc.scalar.copy(out=d_sb[half][:, t, :], in_=d_ps[:])

        def gain_of(half, t):
            return gain_sb[:, span(half * PACK + t, 1)]

        def buyer(half, t):
            a_ps = bank("a_ps", half * PACK + t + 1)
            for a in range(K_PASSES):
                nc.tensor.matmul_mx(out=a_ps[:], lhsT=w1_wo[half][:, span(a * PACK + t, P)].bitcast(FP4X4),
                                    lhsT_scale=w1_so[:, span((a * R_PASSES + half) * PACK + t, P)],
                                    rhs=g_w[a][:].bitcast(FP8X4), rhs_scale=g_sc[a][:],
                                    start=(a == 0), stop=(a == K_PASSES - 1))
            return a_ps

        def times_d(half, t, a_ps):
            nc.vector.scalar_tensor_tensor(out=a_times_d[half][:, t, :], in0=a_ps[:], scalar=gain_of(half, t),
                                           in1=d_sb[half][:, t, :], op0=MULT, op1=MULT)

        def plus_d(half, t, a_ps, staged):
            nc.scalar.copy(out=staged, in_=a_ps[:])
            nc.gpsimd.tensor_tensor(out=a_plus_d(half, t), in0=staged, in1=d_sb[half][:, t, :], op=ADD)

        def plus_d_vector(t):
            nc.vector.tensor_tensor(out=a_plus_d(1, t), in0=a_banks[1, t][:], in1=d_sb[1][:, t, :], op=ADD)

        def seller(half, w2_q):
            banks = [bank("b_ps", 1 + (half * PACK + t) % (BANKS - 1)) for t in range(PACK)]
            for a in range(K_PASSES):
                for t in range(PACK):
                    nc.tensor.matmul_mx(out=banks[t][:], lhsT=w2_q[a][0][:, span(t, P)].bitcast(FP8X4),
                                        lhsT_scale=w2_q[a][1][:, span(t, P)], rhs=g2_w[a][:].bitcast(FP8X4),
                                        rhs_scale=g2_sc[ROWS * (a + 1):, :], start=(a == 0), stop=(a == K_PASSES - 1))
            return banks

        a_banks = {}
        for half in range(R_PASSES):
            for t in range(PACK):
                a_banks[half, t] = buyer(half, t)
        for t in (0, 2):
            plus_d(0, t, a_banks[0, t], a_plus_d(0, t))
        for t in (1, 3, 0, 2):
            times_d(0, t, a_banks[0, t])
        for t in (1, 3):
            plus_d(0, t, a_banks[0, t], a_plus_d(0, t))
        for t in range(PACK):
            times_d(1, t, a_banks[1, t])
        w2_bf = [round_w2(w2_raw[a, 0], f"w2_bf{a}0", None) for a in range(K_PASSES)]

        g2_w = [gather("g2_w0", v2_w[0][:], idx2, U32)]
        w2_q = [quantise("w2_q00", w2_bf[0][:], PASS, "v2_w0")]
        g2_w.append(gather("g2_w1", v2_w[1][:], idx2, U32))
        w2_q.append(quantise("w2_q10", w2_bf[1][:], PASS, "v2_w1"))
        for t in range(2):
            plus_d(1, t, a_banks[1, t], a_sb[:, t, :])
        plus_d_vector(2)
        first_banks = seller(0, w2_q)

        def times_sum(half, banks):
            product = keep.tile([P, PACK, S], F32, name=f"b_times_sum{half}", tag="v_w0" if half == 0 else "w2_raw00",
                                align_bytes=64)
            for t in range(PACK):
                nc.vector.scalar_tensor_tensor(out=product[:, t, :], in0=banks[t][:], scalar=gain_of(half, t),
                                               in1=a_plus_d(half, t), op0=MULT, op1=MULT)
            return product

        def add_up(half, product, js, room=None):
            h_bf = held(f"h_bf{half}_{js.start}", (js.stop - js.start) * PACK, BF16, room)
            nc.vector.tensor_tensor(out=h_bf[:].rearrange("p (c i t) -> p c t i", i=LINE, t=PACK),
                                    in0=product[:, :, js].rearrange("p t (c i) -> p c t i", i=LINE),
                                    in1=a_times_d[half][:, :, js].rearrange("p t (c i) -> p c t i", i=LINE), op=ADD)
            return h_bf

        out_v = out.rearrange("(n p) j -> p n j", p=P)

        def project(part, moving, per_bank, first_bank):
            js = span(part, CHATS)
            banks = [bank("o_ps", first_bank + j) for j in range(N_TILES // per_bank)]
            for half in range(R_PASSES):
                for n in range(N_TILES):
                    i = n % per_bank
                    nc.tensor.matmul_mx(out=banks[n // per_bank][:, span(i, CHATS)],
                                        lhsT=w4_q[half][0][:, span(n, P)].bitcast(FP8X4),
                                        lhsT_scale=w4_q[half][1][:, span(n, P)], rhs=moving[half][0].bitcast(FP8X4),
                                        rhs_scale=moving[half][1], start=(half == 0 and i == 0),
                                        stop=(half == R_PASSES - 1 and i == per_bank - 1))
            for j, o_ps in enumerate(banks):
                o_sb = held(f"o_sb{part}{j}", per_bank * CHATS, F32)
                copy = nc.vector.tensor_copy if per_bank == 1 and j % 2 == 1 else nc.scalar.copy
                copy(out=o_sb[:], in_=o_ps[:, 0:per_bank * CHATS])
                nc.sync.dma_start(out=out_v[:, span(j, per_bank), js],
                                  in_=o_sb[:].rearrange("p (n j) -> p n j", n=per_bank))

        first_product = times_sum(0, first_banks)
        w2_q = [quantise("w2_q01", round_w2(w2_raw[0, 1], "w2_bf01", None)[:], PASS)]
        h_first = [add_up(0, first_product, span(0, CHATS), "w2_raw01")]
        w2_q.append(quantise("w2_q11", round_w2(w2_raw[1, 1], "w2_bf11", None)[:], PASS))
        plus_d_vector(PACK - 1)
        by_slots = keep.tile([P, PACK, CHATS], BF16, name="h_by_slots", tag="w2_bf11", align_bytes=64)
        nc.gpsimd.tensor_tensor(out=by_slots[:], in0=first_product[:, :, span(1, CHATS)],
                                in1=a_times_d[0][:, :, span(1, CHATS)], op=ADD)
        second_product = times_sum(1, seller(1, w2_q))
        w4_bf = [round_w4(w4_raw[half], f"w4_bf{half}") for half in range(R_PASSES)]
        h_first.append(held("h_bf0_woven", CHATS * PACK, BF16, "w4_raw1"))
        nc.scalar.copy(out=h_first[1][:].rearrange("p (c i t) -> p c t i", i=LINE, t=PACK),
                       in_=by_slots[:].rearrange("p t (c i) -> p c t i", i=LINE))

        def moving(h_first_q, h_second_q):
            return [(q[0][:], q[1][:]) for q in (h_first_q, h_second_q)]

        w4_q = [quantise("w4_q0", w4_bf[0][:], N)]
        h_second = add_up(1, second_product, span(0, CHATS), "w4_raw0")
        h_first_q = quantise("h_first_q0", h_first[0][:], CHATS, "w4_bf0")
        w4_q.append(quantise("w4_q1", w4_bf[1][:], N))
        project(0, moving(h_first_q, quantise("h_second_q0", h_second[:], CHATS)), 2, 2)
        h_second = add_up(1, second_product, span(1, CHATS), "w4_bf1")
        h_first_q = quantise("h_first_q1", h_first[1][:], CHATS)
        project(1, moving(h_first_q, quantise("h_second_q1", h_second[:], CHATS)), 1, 4)
